import numpy as np
import ml_dtypes


def mxq(x, axis, fmt="e4m3"):
    dtype, down = {"e4m3": (ml_dtypes.float8_e4m3fn, 7), "e5m2": (ml_dtypes.float8_e5m2, 14)}[fmt]
    v = np.moveaxis(np.asarray(x, np.float32).astype(ml_dtypes.bfloat16).astype(np.float64), axis, -1)
    blocks = v.reshape(v.shape[:-1] + (-1, 32))
    amax = np.abs(blocks).max(-1, keepdims=True)
    byte = np.maximum(np.where(amax > 0, np.frexp(amax)[1] - 1 + 127, 0) - down, 1)
    scale = np.exp2(byte - 127.0)
    codes = (blocks / scale).astype(np.float32).astype(dtype).astype(np.float64)
    return np.moveaxis((codes * scale).reshape(v.shape), -1, axis)


WIDE = False


def mx_kscale(k):
    if not WIDE:
        return np.ones(k)
    levels = np.array([10, -10, 5, -5, 0])
    if k % 512:
        return np.exp2(np.random.permutation(np.resize(levels, k // 32))).repeat(32)
    a = np.empty((k // 512, 16))
    for p in range(k // 512):
        a[p, :8] = np.random.permutation(np.resize(levels, 8))
        for g in range(8):
            far = levels[np.abs(levels - a[p, g]) >= 10]
            a[p, g + 8] = far[np.random.randint(len(far))]
    return np.exp2(a.ravel()).repeat(32)


def f64(x):
    return np.asarray(x).astype(np.float64)


def striped(idx):
    return np.tile(idx.reshape(-1, 16).T, (8, 1)).astype(np.uint16)


def unstriped(offs):
    return offs[:16].T.reshape(-1).astype(np.int64)


def pack_weight(w):
    k, n = w.shape
    w = f64(np.asarray(w, np.float32).astype(ml_dtypes.bfloat16)).reshape(k // 32, 32, n)
    amax = np.abs(w).max(1)
    byte = np.clip(np.where(amax > 0, np.frexp(amax)[1] - 1 + 127 - 7, 1), 1, 254)
    scaled = (w * np.exp2(127.0 - byte)[:, None, :]).reshape(k, n).astype(np.float32)
    words = np.ascontiguousarray(scaled.reshape(k // 512, 128, 4, n).transpose(0, 1, 3, 2)).astype(ml_dtypes.float8_e4m3fn).view(np.uint8)
    return words, np.ascontiguousarray(byte.astype(np.uint8).reshape(k // 512, 16, n))


def unpack_weight(words, scales):
    g, p, n, _ = words.shape
    vals = np.ascontiguousarray(words).view(ml_dtypes.float8_e4m3fn).astype(np.float64) * np.repeat(np.exp2(scales.astype(np.float64) - 127.0), 8, axis=1)[..., None]
    return vals.transpose(0, 1, 3, 2).reshape(g * 512, n)


E2M1 = np.array([0.0, 0.5, 1.0, 1.5, 2.0, 3.0, 4.0, 6.0, -0.0, -0.5, -1.0, -1.5, -2.0, -3.0, -4.0, -6.0])


def pack_fp4(w):
    k, n = w.shape
    w = f64(np.asarray(w, np.float32).astype(ml_dtypes.bfloat16)).reshape(k // 32, 32, n)
    amax = np.abs(w).max(1)
    mant, ex = np.frexp(amax / 6.0)
    byte = np.clip(np.where(amax > 0, np.where(mant > 0.5, ex, ex - 1) + 127, 1), 1, 254)
    scaled = (w * np.exp2(127.0 - byte)[:, None, :]).reshape(k, n).astype(np.float32)
    c = np.ascontiguousarray(scaled.reshape(k // 512, 128, 4, n).transpose(0, 1, 3, 2)).astype(ml_dtypes.float4_e2m1fn).view(np.uint8) & 0xF
    words = (c[..., 0::2] | (c[..., 1::2] << 4)).reshape(k // 512, 128, 2 * n)
    return np.ascontiguousarray(words), np.ascontiguousarray(byte.astype(np.uint8).reshape(k // 512, 16, n))


def unpack_fp4(words, scales):
    g, _, n = scales.shape
    words = np.ascontiguousarray(words).reshape(g, 128, n, 2)
    nib = np.empty((g, 128, n, 4), np.uint8)
    nib[..., 0::2] = words & 0xF
    nib[..., 1::2] = words >> 4
    vals = E2M1[nib] * np.repeat(np.exp2(scales.astype(np.float64) - 127.0), 8, axis=1)[..., None]
    return vals.transpose(0, 1, 3, 2).reshape(g * 512, n)


def planes(y):
    n, m = y.shape
    v = y.astype(np.float32).astype(ml_dtypes.bfloat16).astype(np.float64).reshape(n // 32, 32, m)
    top = np.abs(v).max(1)
    byte = np.clip(np.where(top > 0, np.frexp(top)[1] - 1 + 127 - 7, 1), 1, 254)
    codes = (v * np.exp2(127.0 - byte)[:, None, :]).reshape(n, m).astype(np.float32).astype(ml_dtypes.float8_e4m3fn).view(np.uint8)
    words = codes.reshape(n // 512, 128, 4, m).transpose(0, 1, 3, 2)
    return np.ascontiguousarray(words), np.ascontiguousarray(byte.astype(np.uint8).reshape(n // 512, 16, m))


def relu(v):
    return np.maximum(v, 0.0)


K, T, S, D, V, H, N = 512, 1024, 512, 2, 256, 512, 512
P = 2 ** 7


def setup_inputs():
    n = np.random.standard_normal
    s = mx_kscale(K)[:, None]
    u = mx_kscale(H)
    near = np.random.permutation(S)
    packed_xT = pack_weight(n((K, T)) * s)
    packed_w2 = pack_fp4(n((H, N)) / np.sqrt(2 * H) / u[:, None])
    packed_w3 = pack_fp4(n((K, N)) / np.sqrt(2 * K) / s)
    return {
        "x_words": packed_xT[0],
        "x_scales": packed_xT[1],
        "w1": (n((K, H)) / np.sqrt(K) / s * u).astype(np.float32),
        "w2_words": packed_w2[0],
        "w2_scales": packed_w2[1],
        "gate": (np.tile(np.random.uniform(0.2, 1.0, (D, 1, V)) / np.sqrt(D), (1, P, 1))).astype(np.float32),
        "eT": (n((K, V)) * s).astype(np.float32),
        "w3_words": packed_w3[0],
        "w3_scales": packed_w3[1],
        "offs": striped(np.random.permutation(T)[:S]),
        "pos1": striped(near[:V]),
        "pos2": striped(near[V:]),
    }


def reference(x_words, x_scales, w1, w2_words, w2_scales, gate, eT, w3_words, w3_scales, offs, pos1, pos2):
    xq = unpack_weight(x_words, x_scales)[:, unstriped(offs)]
    h = relu(mxq(f64(w1), 0, "e4m3").T @ xq)
    z = h[:, unstriped(pos1)] * f64(gate)[0, :1] + h[:, unstriped(pos2)] * f64(gate)[1, :1]
    eTq = mxq(f64(eT), 0, "e4m3")
    out_0 = relu(unpack_fp4(w2_words, w2_scales).T @ mxq(z, 0, "e4m3") + unpack_fp4(w3_words, w3_scales).T @ eTq)
    return (out_0,) + planes(out_0)

@@ -1,0 +1,155 @@
+from contextlib import ExitStack
+
+import concourse.mybir as mybir
+
+K, T, S, D, V, H, N = 512, 1024, 512, 2, 256, 512, 512
+FLOPS = 2 * K * H * S + 2 * H * N * V + 2 * K * N * V
+
+F32 = mybir.dt.float32
+BF16 = mybir.dt.bfloat16
+I32 = mybir.dt.int32
+U32 = mybir.dt.uint32
+U16 = mybir.dt.uint16
+U8 = mybir.dt.uint8
+FP8X4 = mybir.dt.float8_e4m3fn_x4
+FP4X4 = mybir.dt.float4_e2m1fn_x4
+RELU = mybir.ActivationFunctionType.Relu
+MULT = mybir.AluOpType.mult
+ADD = mybir.AluOpType.add
+MAX = mybir.AluOpType.max
+
+P = 128
+PACK = 4
+QUADS = 4
+VH = 128
+HALVES = V // VH
+
+
+def tile_picked_zfp_relu_po_kernel(tc, x_words, x_scales, w1, w2_words, w2_scales, gate, eT, w3_words, w3_scales, offs, pos1, pos2, out_0, out_1, out_2):
+    nc = tc.nc
+    with ExitStack() as ctx:
+        sb = ctx.enter_context(tc.tile_pool(name="sb", bufs=1))
+        ps = ctx.enter_context(tc.psum_pool(name="ps", bufs=1))
+
+        def tile(shape, dtype, name):
+            return sb.tile(shape, dtype, name=name, align_bytes=64)
+
+        offs_t = sb.tile([P, S // 16], U16, name="offs_t")
+        pos_t = [sb.tile([P, V // 16], U16, name="pos_t%d" % d) for d in range(D)]
+
+        x_scale_tab = tile([P, T], U8, "x_scale_tab")
+        w_scale_raw = tile([P, 2 * N], U8, "w_scale_raw")
+        warm = tile([P, 8], F32, "warm")
+        warm_out = tile([P, 8], F32, "warm_out")
+        nc.gpsimd.memset(x_scale_tab[:].bitcast(I32), 0)
+        nc.gpsimd.memset(w_scale_raw[:].bitcast(I32), 0)
+        nc.gpsimd.memset(warm[:], 0.0)
+        nc.scalar.activation(warm_out[:], warm[:], RELU)
+
+        x_word_tab = tile([P, T], I32, "x_word_tab")
+        nc.sync.dma_start(x_word_tab[:], x_words[0].rearrange("p c r -> p (c r)").bitcast(I32))
+        for q in range(QUADS):
+            nc.sync.dma_start(x_scale_tab[32 * q : 32 * q + 4, :].bitcast(I32), x_scales[0, 4 * q : 4 * q + 4, :].bitcast(I32))
+        nc.sync.dma_start(offs_t[:], offs)
+        w1_raw = [tile([P, PACK, H // 2], F32, "w1_raw%d" % c) for c in range(2)]
+        w1_rows = w1.rearrange("(p j) c -> p j c", j=PACK)
+        for c in range(2):
+            nc.sync.dma_start(w1_raw[c][:], w1_rows[:, :, c * (H // 2) : (c + 1) * (H // 2)])
+        nc.sync.dma_start(pos_t[0][:], pos1)
+        nc.sync.dma_start(pos_t[1][:], pos2)
+        gate_t = tile([P, D, V], F32, "gate_t")
+        nc.sync.dma_start(gate_t[:], gate.rearrange("d p v -> p d v"))
+        w_word_raw = tile([P, 2, 2 * N], U8, "w_word_raw")
+        nc.sync.dma_start(w_word_raw[:, 0, :], w2_words[0])
+        nc.sync.dma_start(w_word_raw[:, 1, :], w3_words[0])
+        e_raw = tile([P, PACK, V], F32, "e_raw")
+        nc.sync.dma_start(e_raw[:], eT.rearrange("(p j) v -> p j v", j=PACK))
+        for w, scales in enumerate((w2_scales, w3_scales)):
+            for q in range(QUADS):
+                nc.sync.dma_start(w_scale_raw[32 * q : 32 * q + 4, w * N : (w + 1) * N].bitcast(I32), scales[0, 4 * q : 4 * q + 4, :].bitcast(I32))
+
+        x_scale = tile([P, S], U8, "x_scale")
+        x_code = tile([P, S], U32, "x_code")
+        nc.vector.tensor_copy(x_code[:], x_word_tab[:].bitcast(U32).indirect(offs_t[:]))
+        nc.vector.tensor_copy(x_scale[:], x_scale_tab[:].indirect(offs_t[:]))
+
+        w1_bf = tile([P, PACK, P, PACK], BF16, "w1_bf")
+
+        def deal_w1(copy, c, m0, m1):
+            copy(
+                w1_bf[:, :, 64 * c + m0 : 64 * c + m1, :].rearrange("p t m j -> p m j t"),
+                w1_raw[c][:, :, PACK * m0 : PACK * m1].rearrange("p j (m t) -> p m j t", t=PACK),
+            )
+
+        deal_w1(nc.scalar.copy, 0, 0, 64)
+        deal_w1(nc.scalar.copy, 1, 0, 20)
+        deal_w1(nc.vector.tensor_copy, 1, 20, 64)
+
+        banks = [ps.tile([P, S], F32, name="bank%d" % b) for b in range(8)]
+        h = []
+        for t in range(PACK):
+            code = tile([P, P], U32, "w1_code%d" % t)
+            scale = tile([P, P], U8, "w1_scale%d" % t)
+            nc.vector.quantize_mx(code[:].bitcast(FP8X4), scale[:], w1_bf[:, t, :, :].rearrange("p m j -> p (m j)"))
+            nc.tensor.matmul_mx(banks[t][:], lhsT=code[:].bitcast(FP8X4), lhsT_scale=scale[:], rhs=x_code[:].bitcast(FP8X4), rhs_scale=x_scale[:], start=True, stop=True)
+            h_t = tile([P, S], F32, "h%d" % t)
+            nc.scalar.activation(h_t[:], banks[t][:], RELU)
+            h.append(h_t)
+
+        w_code = tile([P, PACK, 2 * P, 2], U8, "w_code")
+        w_scale = tile([P, PACK, 2 * P], U8, "w_scale")
+        nc.vector.tensor_copy(w_code[:], w_word_raw[:].rearrange("p w (m t b) -> p t (w m) b", t=PACK, b=2))
+        nc.vector.tensor_copy(w_scale[:], w_scale_raw[:].rearrange("p (wm t) -> p t wm", t=PACK))
+
+        def weight(w, t):
+            return dict(
+                lhsT=w_code[:, t, w * P : (w + 1) * P, :].rearrange("p m b -> p (m b)").bitcast(FP4X4),
+                lhsT_scale=w_scale[:, t, w * P : (w + 1) * P],
+            )
+
+        e_bf = tile([P, V * PACK], BF16, "e_bf")
+        nc.scalar.copy(e_bf[:].rearrange("p (c i j) -> p c j i", i=4, j=PACK), e_raw[:].rearrange("p j (c i) -> p c j i", i=4))
+        e_code = tile([P, V], U32, "e_code")
+        e_scale = tile([P, V], U8, "e_scale")
+        nc.vector.quantize_mx(e_code[:].bitcast(FP8X4), e_scale[:], e_bf[:])
+
+        y_code = tile([P, V], U32, "y_code")
+        y_scale = tile([P, V], U8, "y_scale")
+        out_rows = out_0.rearrange("(p t) v -> p t v", t=PACK)
+        out_words = out_1[0].rearrange("p c r -> p (c r)").bitcast(I32)
+
+        for u in range(HALVES):
+            cols = slice(u * VH, (u + 1) * VH)
+            acc = [banks[(PACK * (u + 1) + t) % 8][:, 0:VH] for t in range(PACK)]
+            for t in range(PACK):
+                nc.tensor.matmul_mx(acc[t], rhs=e_code[:, cols].bitcast(FP8X4), rhs_scale=e_scale[:, cols], start=True, stop=False, **weight(1, t))
+            part = [tile([P, PACK, VH], F32, "part%d_%d" % (u, d)) for d in range(D)]
+            for t in range(PACK):
+                for d in range(D):
+                    nc.vector.tensor_tensor(part[d][:, t, :], h[t][:].indirect(pos_t[d][:, u * VH // 16 : (u + 1) * VH // 16]), gate_t[:, d, cols], MULT)
+            z_bf = tile([P, VH * PACK], BF16, "z_bf%d" % u)
+            nc.vector.tensor_tensor(
+                z_bf[:].rearrange("p (c i t) -> p c t i", i=4, t=PACK),
+                part[0][:].rearrange("p t (c i) -> p c t i", i=4),
+                part[1][:].rearrange("p t (c i) -> p c t i", i=4),
+                ADD,
+            )
+            z_code = tile([P, VH], U32, "z_code%d" % u)
+            z_scale = tile([P, VH], U8, "z_scale%d" % u)
+            nc.vector.quantize_mx(z_code[:].bitcast(FP8X4), z_scale[:], z_bf[:])
+            y = tile([P, PACK, VH], F32, "y%d" % u)
+            for t in range(PACK):
+                nc.tensor.matmul_mx(acc[t], rhs=z_code[:].bitcast(FP8X4), rhs_scale=z_scale[:], start=False, stop=True, **weight(0, t))
+                if u == HALVES - 1 and t % 2 == 1:
+                    nc.vector.tensor_scalar(y[:, t, :], acc[t], 0.0, None, MAX)
+                else:
+                    nc.scalar.activation(y[:, t, :], acc[t], RELU)
+            nc.sync.dma_start(out_rows[:, :, cols], y[:])
+            y_bf = tile([P, VH * PACK], BF16, "y_bf%d" % u)
+            round_y = nc.vector.tensor_copy if u == HALVES - 1 else nc.scalar.copy
+            round_y(y_bf[:].rearrange("p (c i t) -> p c t i", i=4, t=PACK), y[:].rearrange("p t (c i) -> p c t i", i=4))
+            nc.vector.quantize_mx(y_code[:, cols].bitcast(FP8X4), y_scale[:, cols], y_bf[:])
+            nc.sync.dma_start(out_words[:, cols], y_code[:, cols].bitcast(I32))
+        for q in range(QUADS):
+            queue = nc.scalar if q % 2 == 0 else nc.sync
+            queue.dma_start(out_2[0, 4 * q : 4 * q + 4, :].bitcast(I32), y_scale[32 * q : 32 * q + 4, :].bitcast(I32))

@@ -31,14 +31,14 @@ def tile_picked_zfp_relu_po_kernel(tc, x_words, x_scales, w1, w2_words, w2_scale
         sb = ctx.enter_context(tc.tile_pool(name="sb", bufs=1))
         ps = ctx.enter_context(tc.psum_pool(name="ps", bufs=1))
 
-        def tile(shape, dtype, name):
-            return sb.tile(shape, dtype, name=name, align_bytes=64)
+        def tile(shape, dtype, name, tag=None):
+            return sb.tile(shape, dtype, name=name, tag=tag or name, align_bytes=64)
 
         offs_t = sb.tile([P, S // 16], U16, name="offs_t")
         pos_t = [sb.tile([P, V // 16], U16, name="pos_t%d" % d) for d in range(D)]
 
         x_scale_tab = tile([P, T], U8, "x_scale_tab")
-        w_scale_raw = tile([P, 2 * N], U8, "w_scale_raw")
+        w_scale_raw = tile([P, 2 * N], U8, "w_scale_raw", tag="late1")
         warm = tile([P, 8], F32, "warm")
         warm_out = tile([P, 8], F32, "warm_out")
         nc.gpsimd.memset(x_scale_tab[:].bitcast(I32), 0)
@@ -55,13 +55,13 @@ def tile_picked_zfp_relu_po_kernel(tc, x_words, x_scales, w1, w2_words, w2_scale
         w1_rows = w1.rearrange("(p j) c -> p j c", j=PACK)
         for c in range(2):
             nc.sync.dma_start(w1_raw[c][:], w1_rows[:, :, c * (H // 2) : (c + 1) * (H // 2)])
+        w_word_raw = tile([P, 2, 2 * N], U8, "w_word_raw")
+        nc.sync.dma_start(w_word_raw[:, 0, :], w2_words[0])
+        nc.sync.dma_start(w_word_raw[:, 1, :], w3_words[0])
         nc.sync.dma_start(pos_t[0][:], pos1)
         nc.sync.dma_start(pos_t[1][:], pos2)
         gate_t = tile([P, D, V], F32, "gate_t")
         nc.sync.dma_start(gate_t[:], gate.rearrange("d p v -> p d v"))
-        w_word_raw = tile([P, 2, 2 * N], U8, "w_word_raw")
-        nc.sync.dma_start(w_word_raw[:, 0, :], w2_words[0])
-        nc.sync.dma_start(w_word_raw[:, 1, :], w3_words[0])
         e_raw = tile([P, PACK, V], F32, "e_raw")
         nc.sync.dma_start(e_raw[:], eT.rearrange("(p j) v -> p j v", j=PACK))
         for w, scales in enumerate((w2_scales, w3_scales)):
@@ -82,18 +82,20 @@ def tile_picked_zfp_relu_po_kernel(tc, x_words, x_scales, w1, w2_words, w2_scale
             )
 
         deal_w1(nc.scalar.copy, 0, 0, 64)
-        deal_w1(nc.scalar.copy, 1, 0, 20)
-        deal_w1(nc.vector.tensor_copy, 1, 20, 64)
+        deal_w1(nc.scalar.copy, 1, 0, 16)
+        deal_w1(nc.vector.tensor_copy, 1, 16, 64)
 
         banks = [ps.tile([P, S], F32, name="bank%d" % b) for b in range(8)]
         h = []
         for t in range(PACK):
-            code = tile([P, P], U32, "w1_code%d" % t)
+            code = tile([P, P], U32, "w1_code%d" % t, tag="late0" if t == PACK - 1 else None)
             scale = tile([P, P], U8, "w1_scale%d" % t)
             nc.vector.quantize_mx(code[:].bitcast(FP8X4), scale[:], w1_bf[:, t, :, :].rearrange("p m j -> p (m j)"))
-            nc.tensor.matmul_mx(banks[t][:], lhsT=code[:].bitcast(FP8X4), lhsT_scale=scale[:], rhs=x_code[:].bitcast(FP8X4), rhs_scale=x_scale[:], start=True, stop=True)
             h_t = tile([P, S], F32, "h%d" % t)
-            nc.scalar.activation(h_t[:], banks[t][:], RELU)
+            pieces = [(banks[PACK], slice(0, S // 2)), (banks[0], slice(S // 2, S))] if t == 0 else [(banks[t], slice(0, S))]
+            for bank, cols in pieces:
+                nc.tensor.matmul_mx(bank[:, cols], lhsT=code[:].bitcast(FP8X4), lhsT_scale=scale[:], rhs=x_code[:, cols].bitcast(FP8X4), rhs_scale=x_scale[:, cols], start=True, stop=True)
+                nc.scalar.activation(h_t[:, cols], bank[:, cols], RELU)
             h.append(h_t)
 
         w_code = tile([P, PACK, 2 * P, 2], U8, "w_code")
@@ -107,7 +109,7 @@ def tile_picked_zfp_relu_po_kernel(tc, x_words, x_scales, w1, w2_words, w2_scale
                 lhsT_scale=w_scale[:, t, w * P : (w + 1) * P],
             )
 
-        e_bf = tile([P, V * PACK], BF16, "e_bf")
+        e_bf = tile([P, V * PACK], BF16, "e_bf", tag="late0")
         nc.scalar.copy(e_bf[:].rearrange("p (c i j) -> p c j i", i=4, j=PACK), e_raw[:].rearrange("p j (c i) -> p c j i", i=4))
         e_code = tile([P, V], U32, "e_code")
         e_scale = tile([P, V], U8, "e_scale")
@@ -118,29 +120,31 @@ def tile_picked_zfp_relu_po_kernel(tc, x_words, x_scales, w1, w2_words, w2_scale
         out_rows = out_0.rearrange("(p t) v -> p t v", t=PACK)
         out_words = out_1[0].rearrange("p c r -> p (c r)").bitcast(I32)
 
+        part = [tile([P, PACK, V], F32, "part%d" % d) for d in range(D)]
+        for t in range(PACK):
+            for d in range(D):
+                nc.vector.tensor_tensor(part[d][:, t, :], h[t][:].indirect(pos_t[d][:]), gate_t[:, d, :], MULT)
+
+        z_all = tile([P, V * PACK], BF16, "z_all", tag="late1")
         for u in range(HALVES):
             cols = slice(u * VH, (u + 1) * VH)
             acc = [banks[(PACK * (u + 1) + t) % 8][:, 0:VH] for t in range(PACK)]
             for t in range(PACK):
                 nc.tensor.matmul_mx(acc[t], rhs=e_code[:, cols].bitcast(FP8X4), rhs_scale=e_scale[:, cols], start=True, stop=False, **weight(1, t))
-            part = [tile([P, PACK, VH], F32, "part%d_%d" % (u, d)) for d in range(D)]
-            for t in range(PACK):
-                for d in range(D):
-                    nc.vector.tensor_tensor(part[d][:, t, :], h[t][:].indirect(pos_t[d][:, u * VH // 16 : (u + 1) * VH // 16]), gate_t[:, d, cols], MULT)
-            z_bf = tile([P, VH * PACK], BF16, "z_bf%d" % u)
+            z_bf = z_all[:, u * VH * PACK : (u + 1) * VH * PACK]
             nc.vector.tensor_tensor(
-                z_bf[:].rearrange("p (c i t) -> p c t i", i=4, t=PACK),
-                part[0][:].rearrange("p t (c i) -> p c t i", i=4),
-                part[1][:].rearrange("p t (c i) -> p c t i", i=4),
+                z_bf.rearrange("p (c i t) -> p c t i", i=4, t=PACK),
+                part[0][:, :, cols].rearrange("p t (c i) -> p c t i", i=4),
+                part[1][:, :, cols].rearrange("p t (c i) -> p c t i", i=4),
                 ADD,
             )
             z_code = tile([P, VH], U32, "z_code%d" % u)
             z_scale = tile([P, VH], U8, "z_scale%d" % u)
-            nc.vector.quantize_mx(z_code[:].bitcast(FP8X4), z_scale[:], z_bf[:])
+            nc.vector.quantize_mx(z_code[:].bitcast(FP8X4), z_scale[:], z_bf)
             y = tile([P, PACK, VH], F32, "y%d" % u)
             for t in range(PACK):
                 nc.tensor.matmul_mx(acc[t], rhs=z_code[:].bitcast(FP8X4), rhs_scale=z_scale[:], start=False, stop=True, **weight(0, t))
-                if u == HALVES - 1 and t % 2 == 1:
+                if u == HALVES - 1 or t % 2 == 1:
                     nc.vector.tensor_scalar(y[:, t, :], acc[t], 0.0, None, MAX)
                 else:
                     nc.scalar.activation(y[:, t, :], acc[t], RELU)

@@ -21,8 +21,10 @@ MAX = mybir.AluOpType.max
 P = 128
 PACK = 4
 QUADS = 4
+ROWS = 16
 VH = 128
 HALVES = V // VH
+M_SCALAR = 16
 
 
 def tile_picked_zfp_relu_po_kernel(tc, x_words, x_scales, w1, w2_words, w2_scales, gate, eT, w3_words, w3_scales, offs, pos1, pos2, out_0, out_1, out_2):
@@ -38,35 +40,37 @@ def tile_picked_zfp_relu_po_kernel(tc, x_words, x_scales, w1, w2_words, w2_scale
         pos_t = [sb.tile([P, V // 16], U16, name="pos_t%d" % d) for d in range(D)]
 
         x_scale_tab = tile([P, T], U8, "x_scale_tab")
-        w_scale_raw = tile([P, 2 * N], U8, "w_scale_raw", tag="late1")
+        w_scale_raw = tile([P, N], U8, "w_scale_raw")
+        w_scale = tile([P, 2, PACK, P], U8, "w_scale")
         warm = tile([P, 8], F32, "warm")
         warm_out = tile([P, 8], F32, "warm_out")
-        nc.gpsimd.memset(x_scale_tab[:].bitcast(I32), 0)
-        nc.gpsimd.memset(w_scale_raw[:].bitcast(I32), 0)
-        nc.gpsimd.memset(warm[:], 0.0)
+        nc.vector.memset(x_scale_tab[:].bitcast(I32), 0)
+        nc.vector.memset(warm[:], 0.0)
+        nc.vector.memset(w_scale_raw[:].bitcast(I32), 0)
+        nc.vector.memset(w_scale[:].rearrange("p w t m -> p (w t m)").bitcast(I32), 0)
         nc.scalar.activation(warm_out[:], warm[:], RELU)
 
         x_word_tab = tile([P, T], I32, "x_word_tab")
         nc.sync.dma_start(x_word_tab[:], x_words[0].rearrange("p c r -> p (c r)").bitcast(I32))
+        nc.sync.dma_start(offs_t[:], offs)
         for q in range(QUADS):
             nc.sync.dma_start(x_scale_tab[32 * q : 32 * q + 4, :].bitcast(I32), x_scales[0, 4 * q : 4 * q + 4, :].bitcast(I32))
-        nc.sync.dma_start(offs_t[:], offs)
         w1_raw = [tile([P, PACK, H // 2], F32, "w1_raw%d" % c) for c in range(2)]
         w1_rows = w1.rearrange("(p j) c -> p j c", j=PACK)
         for c in range(2):
             nc.sync.dma_start(w1_raw[c][:], w1_rows[:, :, c * (H // 2) : (c + 1) * (H // 2)])
-        w_word_raw = tile([P, 2, 2 * N], U8, "w_word_raw")
-        nc.sync.dma_start(w_word_raw[:, 0, :], w2_words[0])
-        nc.sync.dma_start(w_word_raw[:, 1, :], w3_words[0])
+        w_word_raw = [tile([P, 2 * N], U8, "w_word_raw%d" % w) for w in range(2)]
+        for w, words in enumerate((w2_words, w3_words)):
+            nc.sync.dma_start(w_word_raw[w][:], words[0])
+        for w, scales in enumerate((w2_scales, w3_scales)):
+            nc.sync.dma_start(w_scale_raw[w : 2 * ROWS : 2, :].bitcast(I32), scales[0].bitcast(I32))
         nc.sync.dma_start(pos_t[0][:], pos1)
         nc.sync.dma_start(pos_t[1][:], pos2)
-        gate_t = tile([P, D, V], F32, "gate_t")
-        nc.sync.dma_start(gate_t[:], gate.rearrange("d p v -> p d v"))
+        gate_t = [tile([P, V], F32, "gate_t%d" % d) for d in range(D)]
+        for d in range(D):
+            nc.sync.dma_start(gate_t[d][:], gate[d])
         e_raw = tile([P, PACK, V], F32, "e_raw")
         nc.sync.dma_start(e_raw[:], eT.rearrange("(p j) v -> p j v", j=PACK))
-        for w, scales in enumerate((w2_scales, w3_scales)):
-            for q in range(QUADS):
-                nc.sync.dma_start(w_scale_raw[32 * q : 32 * q + 4, w * N : (w + 1) * N].bitcast(I32), scales[0, 4 * q : 4 * q + 4, :].bitcast(I32))
 
         x_scale = tile([P, S], U8, "x_scale")
         x_code = tile([P, S], U32, "x_code")
@@ -82,76 +86,86 @@ def tile_picked_zfp_relu_po_kernel(tc, x_words, x_scales, w1, w2_words, w2_scale
             )
 
         deal_w1(nc.scalar.copy, 0, 0, 64)
-        deal_w1(nc.scalar.copy, 1, 0, 16)
-        deal_w1(nc.vector.tensor_copy, 1, 16, 64)
+        deal_w1(nc.scalar.copy, 1, 0, M_SCALAR)
+        deal_w1(nc.vector.tensor_copy, 1, M_SCALAR, 64)
 
+        e_bf = None
         banks = [ps.tile([P, S], F32, name="bank%d" % b) for b in range(8)]
         h = []
         for t in range(PACK):
-            code = tile([P, P], U32, "w1_code%d" % t, tag="late0" if t == PACK - 1 else None)
+            code = tile([P, P], U32, "w1_code%d" % t, tag="late0" if t == PACK - 2 else None)
             scale = tile([P, P], U8, "w1_scale%d" % t)
             nc.vector.quantize_mx(code[:].bitcast(FP8X4), scale[:], w1_bf[:, t, :, :].rearrange("p m j -> p (m j)"))
-            h_t = tile([P, S], F32, "h%d" % t)
+            h_t = tile([P, S], F32, "h%d" % t, tag="e_raw" if t == PACK - 1 else None)
             pieces = [(banks[PACK], slice(0, S // 2)), (banks[0], slice(S // 2, S))] if t == 0 else [(banks[t], slice(0, S))]
             for bank, cols in pieces:
                 nc.tensor.matmul_mx(bank[:, cols], lhsT=code[:].bitcast(FP8X4), lhsT_scale=scale[:], rhs=x_code[:, cols].bitcast(FP8X4), rhs_scale=x_scale[:, cols], start=True, stop=True)
                 nc.scalar.activation(h_t[:, cols], bank[:, cols], RELU)
             h.append(h_t)
+            if t == PACK - 2:
+                e_bf = tile([P, V * PACK], BF16, "e_bf", tag="late0")
+                nc.scalar.copy(e_bf[:].rearrange("p (c i j) -> p c j i", i=4, j=PACK), e_raw[:].rearrange("p j (c i) -> p c j i", i=4))
 
-        w_code = tile([P, PACK, 2 * P, 2], U8, "w_code")
-        w_scale = tile([P, PACK, 2 * P], U8, "w_scale")
-        nc.vector.tensor_copy(w_code[:], w_word_raw[:].rearrange("p w (m t b) -> p t (w m) b", t=PACK, b=2))
-        nc.vector.tensor_copy(w_scale[:], w_scale_raw[:].rearrange("p (wm t) -> p t wm", t=PACK))
-
-        def weight(w, t):
-            return dict(
-                lhsT=w_code[:, t, w * P : (w + 1) * P, :].rearrange("p m b -> p (m b)").bitcast(FP4X4),
-                lhsT_scale=w_scale[:, t, w * P : (w + 1) * P],
+        w_scale_dealt = tile([P, PACK, P], U8, "w_scale_dealt")
+        nc.vector.tensor_copy(w_scale_dealt[:], w_scale_raw[:].rearrange("p (m t) -> p t m", t=PACK))
+        for q in range(QUADS):
+            nc.sync.dma_start(
+                w_scale[32 * q : 32 * q + 4].rearrange("p w t m -> p (w t m)").bitcast(I32),
+                w_scale_dealt[8 * q : 8 * q + 8].rearrange("p t m -> p (t m)").bitcast(I32),
             )
 
-        e_bf = tile([P, V * PACK], BF16, "e_bf", tag="late0")
-        nc.scalar.copy(e_bf[:].rearrange("p (c i j) -> p c j i", i=4, j=PACK), e_raw[:].rearrange("p j (c i) -> p c j i", i=4))
-        e_code = tile([P, V], U32, "e_code")
+        w_code = [tile([P, PACK, P], U16, "w_code%d" % w) for w in range(2)]
+        for w in range(2):
+            nc.vector.tensor_copy(w_code[w][:], w_word_raw[w][:].bitcast(U16).rearrange("p (m t) -> p t m", t=PACK))
+
+        def weight(w, t):
+            return dict(lhsT=w_code[w][:, t].bitcast(FP4X4), lhsT_scale=w_scale[:, w, t, :])
+
+        part = [tile([P, PACK, V], F32, "part%d" % d) for d in range(D)]
+        for t in range(PACK):
+            for d in range(D):
+                nc.vector.tensor_tensor(part[d][:, t, :], h[t][:].indirect(pos_t[d][:]), gate_t[d][:], MULT)
+
+        e_code = tile([P, V], U32, "e_code", tag="gate_t0")
         e_scale = tile([P, V], U8, "e_scale")
         nc.vector.quantize_mx(e_code[:].bitcast(FP8X4), e_scale[:], e_bf[:])
+
+        halves = [slice(u * VH, (u + 1) * VH) for u in range(HALVES)]
+        acc = [[banks[(PACK * (u + 1) + t) % 8][:, 0:VH] for t in range(PACK)] for u in range(HALVES)]
+        for u, cols in enumerate(halves):
+            for t in range(PACK):
+                nc.tensor.matmul_mx(acc[u][t], rhs=e_code[:, cols].bitcast(FP8X4), rhs_scale=e_scale[:, cols], start=True, stop=False, **weight(1, t))
+
+        z_bf = [tile([P, VH * PACK], BF16, "z_bf%d" % u) for u in range(HALVES)]
+        for u, cols in enumerate(halves):
+            nc.vector.tensor_tensor(
+                z_bf[u][:].rearrange("p (c i t) -> p c t i", i=4, t=PACK),
+                part[0][:, :, cols].rearrange("p t (c i) -> p c t i", i=4),
+                part[1][:, :, cols].rearrange("p t (c i) -> p c t i", i=4),
+                ADD,
+            )
+        z_code = [tile([P, VH], U32, "z_code%d" % u) for u in range(HALVES)]
+        z_scale = [tile([P, VH], U8, "z_scale%d" % u) for u in range(HALVES)]
+        for u in range(HALVES):
+            nc.vector.quantize_mx(z_code[u][:].bitcast(FP8X4), z_scale[u][:], z_bf[u][:])
 
         y_code = tile([P, V], U32, "y_code")
         y_scale = tile([P, V], U8, "y_scale")
         out_rows = out_0.rearrange("(p t) v -> p t v", t=PACK)
         out_words = out_1[0].rearrange("p c r -> p (c r)").bitcast(I32)
-
-        part = [tile([P, PACK, V], F32, "part%d" % d) for d in range(D)]
-        for t in range(PACK):
-            for d in range(D):
-                nc.vector.tensor_tensor(part[d][:, t, :], h[t][:].indirect(pos_t[d][:]), gate_t[:, d, :], MULT)
-
-        z_all = tile([P, V * PACK], BF16, "z_all", tag="late1")
-        for u in range(HALVES):
-            cols = slice(u * VH, (u + 1) * VH)
-            acc = [banks[(PACK * (u + 1) + t) % 8][:, 0:VH] for t in range(PACK)]
+        y = [tile([P, PACK, VH], F32, "y%d" % u) for u in range(HALVES)]
+        for u, cols in enumerate(halves):
             for t in range(PACK):
-                nc.tensor.matmul_mx(acc[t], rhs=e_code[:, cols].bitcast(FP8X4), rhs_scale=e_scale[:, cols], start=True, stop=False, **weight(1, t))
-            z_bf = z_all[:, u * VH * PACK : (u + 1) * VH * PACK]
-            nc.vector.tensor_tensor(
-                z_bf.rearrange("p (c i t) -> p c t i", i=4, t=PACK),
-                part[0][:, :, cols].rearrange("p t (c i) -> p c t i", i=4),
-                part[1][:, :, cols].rearrange("p t (c i) -> p c t i", i=4),
-                ADD,
-            )
-            z_code = tile([P, VH], U32, "z_code%d" % u)
-            z_scale = tile([P, VH], U8, "z_scale%d" % u)
-            nc.vector.quantize_mx(z_code[:].bitcast(FP8X4), z_scale[:], z_bf)
-            y = tile([P, PACK, VH], F32, "y%d" % u)
-            for t in range(PACK):
-                nc.tensor.matmul_mx(acc[t], rhs=z_code[:].bitcast(FP8X4), rhs_scale=z_scale[:], start=False, stop=True, **weight(0, t))
-                if u == HALVES - 1 or t % 2 == 1:
-                    nc.vector.tensor_scalar(y[:, t, :], acc[t], 0.0, None, MAX)
+                nc.tensor.matmul_mx(acc[u][t], rhs=z_code[u][:].bitcast(FP8X4), rhs_scale=z_scale[u][:], start=False, stop=True, **weight(0, t))
+                if u == 0 and t % 2 == 0:
+                    nc.vector.tensor_scalar(y[u][:, t, :], acc[u][t], 0.0, None, MAX)
                 else:
-                    nc.scalar.activation(y[:, t, :], acc[t], RELU)
-            nc.sync.dma_start(out_rows[:, :, cols], y[:])
+                    nc.scalar.activation(y[u][:, t, :], acc[u][t], RELU)
+            queue = nc.sync if u == 0 else nc.scalar
+            queue.dma_start(out_rows[:, :, cols], y[u][:])
+        for u, cols in enumerate(halves):
             y_bf = tile([P, VH * PACK], BF16, "y_bf%d" % u)
-            round_y = nc.vector.tensor_copy if u == HALVES - 1 else nc.scalar.copy
-            round_y(y_bf[:].rearrange("p (c i t) -> p c t i", i=4, t=PACK), y[:].rearrange("p t (c i) -> p c t i", i=4))
+            nc.vector.tensor_copy(y_bf[:].rearrange("p (c i t) -> p c t i", i=4, t=PACK), y[u][:].rearrange("p t (c i) -> p c t i", i=4))
             nc.vector.quantize_mx(y_code[:, cols].bitcast(FP8X4), y_scale[:, cols], y_bf[:])
             nc.sync.dma_start(out_words[:, cols], y_code[:, cols].bitcast(I32))
         for q in range(QUADS):

@@ -14,6 +14,7 @@ U8 = mybir.dt.uint8
 FP8X4 = mybir.dt.float8_e4m3fn_x4
 FP4X4 = mybir.dt.float4_e2m1fn_x4
 RELU = mybir.ActivationFunctionType.Relu
+COPY = mybir.ActivationFunctionType.Copy
 MULT = mybir.AluOpType.mult
 ADD = mybir.AluOpType.add
 MAX = mybir.AluOpType.max
@@ -24,13 +25,14 @@ QUADS = 4
 ROWS = 16
 VH = 128
 HALVES = V // VH
-M_SCALAR = 16
+M_SCALAR = 24
 
 
 def tile_picked_zfp_relu_po_kernel(tc, x_words, x_scales, w1, w2_words, w2_scales, gate, eT, w3_words, w3_scales, offs, pos1, pos2, out_0, out_1, out_2):
     nc = tc.nc
     with ExitStack() as ctx:
         sb = ctx.enter_context(tc.tile_pool(name="sb", bufs=1))
+        over = ctx.enter_context(tc.tile_pool(name="over", bufs=1))
         ps = ctx.enter_context(tc.psum_pool(name="ps", bufs=1))
 
         def tile(shape, dtype, name, tag=None):
@@ -42,20 +44,16 @@ def tile_picked_zfp_relu_po_kernel(tc, x_words, x_scales, w1, w2_words, w2_scale
         x_scale_tab = tile([P, T], U8, "x_scale_tab")
         w_scale_raw = tile([P, N], U8, "w_scale_raw")
         w_scale = tile([P, 2, PACK, P], U8, "w_scale")
-        warm = tile([P, 8], F32, "warm")
-        warm_out = tile([P, 8], F32, "warm_out")
         nc.vector.memset(x_scale_tab[:].bitcast(I32), 0)
-        nc.vector.memset(warm[:], 0.0)
         nc.vector.memset(w_scale_raw[:].bitcast(I32), 0)
         nc.vector.memset(w_scale[:].rearrange("p w t m -> p (w t m)").bitcast(I32), 0)
-        nc.scalar.activation(warm_out[:], warm[:], RELU)
 
         x_word_tab = tile([P, T], I32, "x_word_tab")
         nc.sync.dma_start(x_word_tab[:], x_words[0].rearrange("p c r -> p (c r)").bitcast(I32))
         nc.sync.dma_start(offs_t[:], offs)
         for q in range(QUADS):
             nc.sync.dma_start(x_scale_tab[32 * q : 32 * q + 4, :].bitcast(I32), x_scales[0, 4 * q : 4 * q + 4, :].bitcast(I32))
-        w1_raw = [tile([P, PACK, H // 2], F32, "w1_raw%d" % c) for c in range(2)]
+        w1_raw = [tile([P, PACK, H // 2], F32, "w1_raw0"), over.tile([P, PACK, H // 2], F32, name="w1_raw1", offset=0, align_bytes=64)]
         w1_rows = w1.rearrange("(p j) c -> p j c", j=PACK)
         for c in range(2):
             nc.sync.dma_start(w1_raw[c][:], w1_rows[:, :, c * (H // 2) : (c + 1) * (H // 2)])
@@ -85,7 +83,7 @@ def tile_picked_zfp_relu_po_kernel(tc, x_words, x_scales, w1, w2_words, w2_scale
                 w1_raw[c][:, :, PACK * m0 : PACK * m1].rearrange("p j (m t) -> p m j t", t=PACK),
             )
 
-        deal_w1(nc.scalar.copy, 0, 0, 64)
+        deal_w1(lambda out, in_: nc.scalar.activation(out, in_, COPY), 0, 0, 64)
         deal_w1(nc.scalar.copy, 1, 0, M_SCALAR)
         deal_w1(nc.vector.tensor_copy, 1, M_SCALAR, 64)
 
@@ -114,7 +112,7 @@ def tile_picked_zfp_relu_po_kernel(tc, x_words, x_scales, w1, w2_words, w2_scale
                 w_scale_dealt[8 * q : 8 * q + 8].rearrange("p t m -> p (t m)").bitcast(I32),
             )
 
-        w_code = [tile([P, PACK, P], U16, "w_code%d" % w) for w in range(2)]
+        w_code = [over.tile([P, PACK, P], U16, name="w_code%d" % w, offset=w * 2 * N, align_bytes=64) for w in range(2)]
         for w in range(2):
             nc.vector.tensor_copy(w_code[w][:], w_word_raw[w][:].bitcast(U16).rearrange("p (m t) -> p t m", t=PACK))
 
@@ -157,16 +155,17 @@ def tile_picked_zfp_relu_po_kernel(tc, x_words, x_scales, w1, w2_words, w2_scale
         for u, cols in enumerate(halves):
             for t in range(PACK):
                 nc.tensor.matmul_mx(acc[u][t], rhs=z_code[u][:].bitcast(FP8X4), rhs_scale=z_scale[u][:], start=False, stop=True, **weight(0, t))
-                if u == 0 and t % 2 == 0:
+                if (u == 0 and t % 2 == 0) or (u == 1 and t == 0):
                     nc.vector.tensor_scalar(y[u][:, t, :], acc[u][t], 0.0, None, MAX)
                 else:
                     nc.scalar.activation(y[u][:, t, :], acc[u][t], RELU)
             queue = nc.sync if u == 0 else nc.scalar
             queue.dma_start(out_rows[:, :, cols], y[u][:])
+        y_bf = [tile([P, VH * PACK], BF16, "y_bf%d" % u) for u in range(HALVES)]
+        for u in range(HALVES):
+            nc.vector.tensor_copy(y_bf[u][:].rearrange("p (c i t) -> p c t i", i=4, t=PACK), y[u][:].rearrange("p t (c i) -> p c t i", i=4))
         for u, cols in enumerate(halves):
-            y_bf = tile([P, VH * PACK], BF16, "y_bf%d" % u)
-            nc.vector.tensor_copy(y_bf[:].rearrange("p (c i t) -> p c t i", i=4, t=PACK), y[u][:].rearrange("p t (c i) -> p c t i", i=4))
-            nc.vector.quantize_mx(y_code[:, cols].bitcast(FP8X4), y_scale[:, cols], y_bf[:])
+            nc.vector.quantize_mx(y_code[:, cols].bitcast(FP8X4), y_scale[:, cols], y_bf[u][:])
             nc.sync.dma_start(out_words[:, cols], y_code[:, cols].bitcast(I32))
         for q in range(QUADS):
             queue = nc.scalar if q % 2 == 0 else nc.sync

@@ -25,7 +25,6 @@ QUADS = 4
 ROWS = 16
 VH = 128
 HALVES = V // VH
-M_SCALAR = 24
 
 
 def tile_picked_zfp_relu_po_kernel(tc, x_words, x_scales, w1, w2_words, w2_scales, gate, eT, w3_words, w3_scales, offs, pos1, pos2, out_0, out_1, out_2):
@@ -75,17 +74,18 @@ def tile_picked_zfp_relu_po_kernel(tc, x_words, x_scales, w1, w2_words, w2_scale
         nc.vector.tensor_copy(x_code[:], x_word_tab[:].bitcast(U32).indirect(offs_t[:]))
         nc.vector.tensor_copy(x_scale[:], x_scale_tab[:].indirect(offs_t[:]))
 
-        w1_bf = tile([P, PACK, P, PACK], BF16, "w1_bf")
+        w1_bf = [tile([P, 2, P, PACK], BF16, "w1_bf%d" % a) for a in range(2)]
 
-        def deal_w1(copy, c, m0, m1):
+        def deal_w1(copy, a, c):
             copy(
-                w1_bf[:, :, 64 * c + m0 : 64 * c + m1, :].rearrange("p t m j -> p m j t"),
-                w1_raw[c][:, :, PACK * m0 : PACK * m1].rearrange("p j (m t) -> p m j t", t=PACK),
+                w1_bf[a][:, :, 64 * c : 64 * (c + 1), :].rearrange("p b m j -> p m j b"),
+                w1_raw[c][:].rearrange("p j (m t) -> p m j t", t=PACK)[:, :, :, 2 * a : 2 * a + 2],
             )
 
-        deal_w1(lambda out, in_: nc.scalar.activation(out, in_, COPY), 0, 0, 64)
-        deal_w1(nc.scalar.copy, 1, 0, M_SCALAR)
-        deal_w1(nc.vector.tensor_copy, 1, M_SCALAR, 64)
+        deal_w1(lambda out, in_: nc.scalar.activation(out, in_, COPY), 0, 0)
+        deal_w1(nc.scalar.copy, 1, 0)
+        deal_w1(nc.vector.tensor_copy, 0, 1)
+        deal_w1(nc.scalar.copy, 1, 1)
 
         e_bf = None
         banks = [ps.tile([P, S], F32, name="bank%d" % b) for b in range(8)]
@@ -93,7 +93,7 @@ def tile_picked_zfp_relu_po_kernel(tc, x_words, x_scales, w1, w2_words, w2_scale
         for t in range(PACK):
             code = tile([P, P], U32, "w1_code%d" % t, tag="late0" if t == PACK - 2 else None)
             scale = tile([P, P], U8, "w1_scale%d" % t)
-            nc.vector.quantize_mx(code[:].bitcast(FP8X4), scale[:], w1_bf[:, t, :, :].rearrange("p m j -> p (m j)"))
+            nc.vector.quantize_mx(code[:].bitcast(FP8X4), scale[:], w1_bf[t // 2][:, t % 2].rearrange("p m j -> p (m j)"))
             h_t = tile([P, S], F32, "h%d" % t, tag="e_raw" if t == PACK - 1 else None)
             pieces = [(banks[PACK], slice(0, S // 2)), (banks[0], slice(S // 2, S))] if t == 0 else [(banks[t], slice(0, S))]
             for bank, cols in pieces:

@@ -23,8 +23,11 @@ P = 128
 PACK = 4
 QUADS = 4
 ROWS = 16
+RUN = 4
 VH = 128
 HALVES = V // VH
+W2, W3 = 0, 1
+AT_W3_CODE, AT_W_SCALE, AT_W1_SCALE = 0, 2 * N, 3 * N
 
 
 def tile_picked_zfp_relu_po_kernel(tc, x_words, x_scales, w1, w2_words, w2_scales, gate, eT, w3_words, w3_scales, offs, pos1, pos2, out_0, out_1, out_2):
@@ -36,6 +39,9 @@ def tile_picked_zfp_relu_po_kernel(tc, x_words, x_scales, w1, w2_words, w2_scale
 
         def tile(shape, dtype, name, tag=None):
             return sb.tile(shape, dtype, name=name, tag=tag or name, align_bytes=64)
+
+        def on_raw_w1(shape, dtype, name, offset):
+            return over.tile(shape, dtype, name=name, offset=offset, align_bytes=64)
 
         offs_t = sb.tile([P, S // 16], U16, name="offs_t")
         pos_t = [sb.tile([P, V // 16], U16, name="pos_t%d" % d) for d in range(D)]
@@ -52,14 +58,14 @@ def tile_picked_zfp_relu_po_kernel(tc, x_words, x_scales, w1, w2_words, w2_scale
         nc.sync.dma_start(offs_t[:], offs)
         for q in range(QUADS):
             nc.sync.dma_start(x_scale_tab[32 * q : 32 * q + 4, :].bitcast(I32), x_scales[0, 4 * q : 4 * q + 4, :].bitcast(I32))
-        w1_raw = [tile([P, PACK, H // 2], F32, "w1_raw0"), over.tile([P, PACK, H // 2], F32, name="w1_raw1", offset=0, align_bytes=64)]
+        w1_raw = [tile([P, PACK, H // 2], F32, "w1_raw0"), on_raw_w1([P, PACK, H // 2], F32, "w1_raw1", 0)]
         w1_rows = w1.rearrange("(p j) c -> p j c", j=PACK)
         for c in range(2):
             nc.sync.dma_start(w1_raw[c][:], w1_rows[:, :, c * (H // 2) : (c + 1) * (H // 2)])
-        w_word_raw = [tile([P, 2 * N], U8, "w_word_raw%d" % w) for w in range(2)]
-        for w, words in enumerate((w2_words, w3_words)):
+        w_word_raw = [tile([P, 2 * N], U8, "w_word_raw%d" % w) for w in (W2, W3)]
+        for w, words in ((W2, w2_words), (W3, w3_words)):
             nc.sync.dma_start(w_word_raw[w][:], words[0])
-        for w, scales in enumerate((w2_scales, w3_scales)):
+        for w, scales in ((W2, w2_scales), (W3, w3_scales)):
             nc.sync.dma_start(w_scale_raw[w : 2 * ROWS : 2, :].bitcast(I32), scales[0].bitcast(I32))
         nc.sync.dma_start(pos_t[0][:], pos1)
         nc.sync.dma_start(pos_t[1][:], pos2)
@@ -78,42 +84,43 @@ def tile_picked_zfp_relu_po_kernel(tc, x_words, x_scales, w1, w2_words, w2_scale
 
         def deal_w1(copy, a, c):
             copy(
-                w1_bf[a][:, :, 64 * c : 64 * (c + 1), :].rearrange("p b m j -> p m j b"),
+                w1_bf[a][:, :, P // 2 * c : P // 2 * (c + 1), :].rearrange("p b m j -> p m j b"),
                 w1_raw[c][:].rearrange("p j (m t) -> p m j t", t=PACK)[:, :, :, 2 * a : 2 * a + 2],
             )
 
         deal_w1(lambda out, in_: nc.scalar.activation(out, in_, COPY), 0, 0)
         deal_w1(nc.scalar.copy, 1, 0)
-        deal_w1(nc.vector.tensor_copy, 0, 1)
-        deal_w1(nc.scalar.copy, 1, 1)
+        deal_w1(nc.scalar.copy, 0, 1)
+        deal_w1(nc.vector.tensor_copy, 1, 1)
 
-        e_bf = None
         banks = [ps.tile([P, S], F32, name="bank%d" % b) for b in range(8)]
-        h = []
-        for t in range(PACK):
-            code = tile([P, P], U32, "w1_code%d" % t, tag="late0" if t == PACK - 2 else None)
-            scale = tile([P, P], U8, "w1_scale%d" % t)
+
+        def make_h(t, code_tag=None, h_tag=None):
+            code = tile([P, P], U32, "w1_code%d" % t, tag=code_tag)
+            name = "w1_scale%d" % t
+            scale = tile([P, P], U8, name) if t < 2 else on_raw_w1([P, P], U8, name, AT_W1_SCALE + (t - 2) * P)
             nc.vector.quantize_mx(code[:].bitcast(FP8X4), scale[:], w1_bf[t // 2][:, t % 2].rearrange("p m j -> p (m j)"))
-            h_t = tile([P, S], F32, "h%d" % t, tag="e_raw" if t == PACK - 1 else None)
+            h_t = tile([P, S], F32, "h%d" % t, tag=h_tag)
             pieces = [(banks[PACK], slice(0, S // 2)), (banks[0], slice(S // 2, S))] if t == 0 else [(banks[t], slice(0, S))]
             for bank, cols in pieces:
                 nc.tensor.matmul_mx(bank[:, cols], lhsT=code[:].bitcast(FP8X4), lhsT_scale=scale[:], rhs=x_code[:, cols].bitcast(FP8X4), rhs_scale=x_scale[:, cols], start=True, stop=True)
                 nc.scalar.activation(h_t[:, cols], bank[:, cols], RELU)
-            h.append(h_t)
-            if t == PACK - 2:
-                e_bf = tile([P, V * PACK], BF16, "e_bf", tag="late0")
-                nc.scalar.copy(e_bf[:].rearrange("p (c i j) -> p c j i", i=4, j=PACK), e_raw[:].rearrange("p j (c i) -> p c j i", i=4))
+            return h_t
 
-        w_scale_dealt = tile([P, PACK, P], U8, "w_scale_dealt")
+        h = [make_h(0), make_h(1), make_h(2, code_tag="e_bf")]
+        e_bf = tile([P, V * PACK], BF16, "e_bf")
+        nc.scalar.copy(e_bf[:].rearrange("p (c i j) -> p c j i", i=RUN, j=PACK), e_raw[:].rearrange("p j (c i) -> p c j i", i=RUN))
+        h.append(make_h(3, h_tag="e_raw"))
+
+        w_scale_dealt = on_raw_w1([P, PACK, P], U8, "w_scale_dealt", AT_W_SCALE)
         nc.vector.tensor_copy(w_scale_dealt[:], w_scale_raw[:].rearrange("p (m t) -> p t m", t=PACK))
         for q in range(QUADS):
             nc.sync.dma_start(
                 w_scale[32 * q : 32 * q + 4].rearrange("p w t m -> p (w t m)").bitcast(I32),
                 w_scale_dealt[8 * q : 8 * q + 8].rearrange("p t m -> p (t m)").bitcast(I32),
             )
-
-        w_code = [over.tile([P, PACK, P], U16, name="w_code%d" % w, offset=w * 2 * N, align_bytes=64) for w in range(2)]
-        for w in range(2):
+        w_code = [tile([P, PACK, P], U16, "w2_code"), on_raw_w1([P, PACK, P], U16, "w3_code", AT_W3_CODE)]
+        for w in (W2, W3):
             nc.vector.tensor_copy(w_code[w][:], w_word_raw[w][:].bitcast(U16).rearrange("p (m t) -> p t m", t=PACK))
 
         def weight(w, t):
@@ -132,14 +139,14 @@ def tile_picked_zfp_relu_po_kernel(tc, x_words, x_scales, w1, w2_words, w2_scale
         acc = [[banks[(PACK * (u + 1) + t) % 8][:, 0:VH] for t in range(PACK)] for u in range(HALVES)]
         for u, cols in enumerate(halves):
             for t in range(PACK):
-                nc.tensor.matmul_mx(acc[u][t], rhs=e_code[:, cols].bitcast(FP8X4), rhs_scale=e_scale[:, cols], start=True, stop=False, **weight(1, t))
+                nc.tensor.matmul_mx(acc[u][t], rhs=e_code[:, cols].bitcast(FP8X4), rhs_scale=e_scale[:, cols], start=True, stop=False, **weight(W3, t))
 
         z_bf = [tile([P, VH * PACK], BF16, "z_bf%d" % u) for u in range(HALVES)]
         for u, cols in enumerate(halves):
             nc.vector.tensor_tensor(
-                z_bf[u][:].rearrange("p (c i t) -> p c t i", i=4, t=PACK),
-                part[0][:, :, cols].rearrange("p t (c i) -> p c t i", i=4),
-                part[1][:, :, cols].rearrange("p t (c i) -> p c t i", i=4),
+                z_bf[u][:].rearrange("p (c i t) -> p c t i", i=RUN, t=PACK),
+                part[0][:, :, cols].rearrange("p t (c i) -> p c t i", i=RUN),
+                part[1][:, :, cols].rearrange("p t (c i) -> p c t i", i=RUN),
                 ADD,
             )
         z_code = [tile([P, VH], U32, "z_code%d" % u) for u in range(HALVES)]
@@ -154,16 +161,17 @@ def tile_picked_zfp_relu_po_kernel(tc, x_words, x_scales, w1, w2_words, w2_scale
         y = [tile([P, PACK, VH], F32, "y%d" % u) for u in range(HALVES)]
         for u, cols in enumerate(halves):
             for t in range(PACK):
-                nc.tensor.matmul_mx(acc[u][t], rhs=z_code[u][:].bitcast(FP8X4), rhs_scale=z_scale[u][:], start=False, stop=True, **weight(0, t))
+                nc.tensor.matmul_mx(acc[u][t], rhs=z_code[u][:].bitcast(FP8X4), rhs_scale=z_scale[u][:], start=False, stop=True, **weight(W2, t))
                 if (u == 0 and t % 2 == 0) or (u == 1 and t == 0):
                     nc.vector.tensor_scalar(y[u][:, t, :], acc[u][t], 0.0, None, MAX)
                 else:
                     nc.scalar.activation(y[u][:, t, :], acc[u][t], RELU)
             queue = nc.sync if u == 0 else nc.scalar
             queue.dma_start(out_rows[:, :, cols], y[u][:])
+
         y_bf = [tile([P, VH * PACK], BF16, "y_bf%d" % u) for u in range(HALVES)]
         for u in range(HALVES):
-            nc.vector.tensor_copy(y_bf[u][:].rearrange("p (c i t) -> p c t i", i=4, t=PACK), y[u][:].rearrange("p t (c i) -> p c t i", i=4))
+            nc.vector.tensor_copy(y_bf[u][:].rearrange("p (c i t) -> p c t i", i=RUN, t=PACK), y[u][:].rearrange("p t (c i) -> p c t i", i=RUN))
         for u, cols in enumerate(halves):
             nc.vector.quantize_mx(y_code[:, cols].bitcast(FP8X4), y_scale[:, cols], y_bf[u][:])
             nc.sync.dma_start(out_words[:, cols], y_code[:, cols].bitcast(I32))

@@ -49,9 +49,9 @@ def tile_picked_zfp_relu_po_kernel(tc, x_words, x_scales, w1, w2_words, w2_scale
         x_scale_tab = tile([P, T], U8, "x_scale_tab")
         w_scale_raw = tile([P, N], U8, "w_scale_raw")
         w_scale = tile([P, 2, PACK, P], U8, "w_scale")
-        nc.vector.memset(x_scale_tab[:].bitcast(I32), 0)
-        nc.vector.memset(w_scale_raw[:].bitcast(I32), 0)
-        nc.vector.memset(w_scale[:].rearrange("p w t m -> p (w t m)").bitcast(I32), 0)
+        nc.gpsimd.memset(x_scale_tab[:].bitcast(I32), 0)
+        nc.gpsimd.memset(w_scale_raw[:].bitcast(I32), 0)
+        nc.gpsimd.memset(w_scale[:].rearrange("p w t m -> p (w t m)").bitcast(I32), 0)
 
         x_word_tab = tile([P, T], I32, "x_word_tab")
         nc.sync.dma_start(x_word_tab[:], x_words[0].rearrange("p c r -> p (c r)").bitcast(I32))
@@ -127,16 +127,25 @@ def tile_picked_zfp_relu_po_kernel(tc, x_words, x_scales, w1, w2_words, w2_scale
             return dict(lhsT=w_code[w][:, t].bitcast(FP4X4), lhsT_scale=w_scale[:, w, t, :])
 
         part = [tile([P, PACK, V], F32, "part%d" % d) for d in range(D)]
-        for t in range(PACK):
-            for d in range(D):
-                nc.vector.tensor_tensor(part[d][:, t, :], h[t][:].indirect(pos_t[d][:]), gate_t[d][:], MULT)
+        halves = [slice(u * VH, (u + 1) * VH) for u in range(HALVES)]
 
-        e_code = tile([P, V], U32, "e_code", tag="gate_t0")
+        def gather(t, d, cols):
+            offsets = pos_t[d][:, cols.start // 16 : cols.stop // 16]
+            nc.vector.tensor_tensor(part[d][:, t, cols], h[t][:].indirect(offsets), gate_t[d][:, cols], MULT)
+
+        for t in range(PACK - 1):
+            for d in range(D):
+                gather(t, d, slice(0, V))
+        e_code = tile([P, V], U32, "e_code", tag="w_word_raw%d" % W3)
         e_scale = tile([P, V], U8, "e_scale")
         nc.vector.quantize_mx(e_code[:].bitcast(FP8X4), e_scale[:], e_bf[:])
+        gather(PACK - 1, 0, slice(0, V))
+        for cols in halves:
+            gather(PACK - 1, 1, cols)
 
-        halves = [slice(u * VH, (u + 1) * VH) for u in range(HALVES)]
         acc = [[banks[(PACK * (u + 1) + t) % 8][:, 0:VH] for t in range(PACK)] for u in range(HALVES)]
+        for bank, cols in ((banks[7], slice(0, V)), (banks[6], halves[0])):
+            nc.tensor.matmul_mx(bank[:, cols], rhs=e_code[:, cols].bitcast(FP8X4), rhs_scale=e_scale[:, cols], start=True, stop=True, **weight(W3, 0))
         for u, cols in enumerate(halves):
             for t in range(PACK):
                 nc.tensor.matmul_mx(acc[u][t], rhs=e_code[:, cols].bitcast(FP8X4), rhs_scale=e_scale[:, cols], start=True, stop=False, **weight(W3, t))
@@ -162,7 +171,7 @@ def tile_picked_zfp_relu_po_kernel(tc, x_words, x_scales, w1, w2_words, w2_scale
         for u, cols in enumerate(halves):
             for t in range(PACK):
                 nc.tensor.matmul_mx(acc[u][t], rhs=z_code[u][:].bitcast(FP8X4), rhs_scale=z_scale[u][:], start=False, stop=True, **weight(W2, t))
-                if (u == 0 and t % 2 == 0) or (u == 1 and t == 0):
+                if t % 2 == 0:
                     nc.vector.tensor_scalar(y[u][:, t, :], acc[u][t], 0.0, None, MAX)
                 else:
                     nc.scalar.activation(y[u][:, t, :], acc[u][t], RELU)

@@ -35,6 +35,7 @@ def tile_picked_zfp_relu_po_kernel(tc, x_words, x_scales, w1, w2_words, w2_scale
     with ExitStack() as ctx:
         sb = ctx.enter_context(tc.tile_pool(name="sb", bufs=1))
         over = ctx.enter_context(tc.tile_pool(name="over", bufs=1))
+        over_e = ctx.enter_context(tc.tile_pool(name="over_e", bufs=1))
         ps = ctx.enter_context(tc.psum_pool(name="ps", bufs=1))
 
         def tile(shape, dtype, name, tag=None):
@@ -69,11 +70,13 @@ def tile_picked_zfp_relu_po_kernel(tc, x_words, x_scales, w1, w2_words, w2_scale
             nc.sync.dma_start(w_scale_raw[w : 2 * ROWS : 2, :].bitcast(I32), scales[0].bitcast(I32))
         nc.sync.dma_start(pos_t[0][:], pos1)
         nc.sync.dma_start(pos_t[1][:], pos2)
-        gate_t = [tile([P, V], F32, "gate_t%d" % d) for d in range(D)]
-        for d in range(D):
-            nc.sync.dma_start(gate_t[d][:], gate[d])
-        e_raw = tile([P, PACK, V], F32, "e_raw")
-        nc.sync.dma_start(e_raw[:], eT.rearrange("(p j) v -> p j v", j=PACK))
+        gates = tile([P, D, V], F32, "gates")
+        nc.sync.dma_start(gates[:], gate.rearrange("d p v -> p d v"))
+        gate_t = [gates[:, d, :] for d in range(D)]
+        e_rows = eT.rearrange("(p j) v -> p j v", j=PACK)
+        e_raw = [over_e.tile([P, PACK, VH], F32, name="e_raw0", offset=0, align_bytes=64)[:], tile([P, PACK, VH], F32, "e_raw1")[:]]
+        for u in range(HALVES):
+            nc.sync.dma_start(e_raw[u], e_rows[:, :, u * VH : (u + 1) * VH])
 
         x_scale = tile([P, S], U8, "x_scale")
         x_code = tile([P, S], U32, "x_code")
@@ -101,16 +104,13 @@ def tile_picked_zfp_relu_po_kernel(tc, x_words, x_scales, w1, w2_words, w2_scale
             scale = tile([P, P], U8, name) if t < 2 else on_raw_w1([P, P], U8, name, AT_W1_SCALE + (t - 2) * P)
             nc.vector.quantize_mx(code[:].bitcast(FP8X4), scale[:], w1_bf[t // 2][:, t % 2].rearrange("p m j -> p (m j)"))
             h_t = tile([P, S], F32, "h%d" % t, tag=h_tag)
-            pieces = [(banks[PACK], slice(0, S // 2)), (banks[0], slice(S // 2, S))] if t == 0 else [(banks[t], slice(0, S))]
-            for bank, cols in pieces:
+            for c in range(2):
+                bank, cols = banks[2 * t + c], slice(c * S // 2, (c + 1) * S // 2)
                 nc.tensor.matmul_mx(bank[:, cols], lhsT=code[:].bitcast(FP8X4), lhsT_scale=scale[:], rhs=x_code[:, cols].bitcast(FP8X4), rhs_scale=x_scale[:, cols], start=True, stop=True)
                 nc.scalar.activation(h_t[:, cols], bank[:, cols], RELU)
             return h_t
 
-        h = [make_h(0), make_h(1), make_h(2, code_tag="e_bf")]
-        e_bf = tile([P, V * PACK], BF16, "e_bf")
-        nc.scalar.copy(e_bf[:].rearrange("p (c i j) -> p c j i", i=RUN, j=PACK), e_raw[:].rearrange("p j (c i) -> p c j i", i=RUN))
-        h.append(make_h(3, h_tag="e_raw"))
+        h = [make_h(t) for t in range(PACK)]
 
         w_scale_dealt = on_raw_w1([P, PACK, P], U8, "w_scale_dealt", AT_W_SCALE)
         nc.vector.tensor_copy(w_scale_dealt[:], w_scale_raw[:].rearrange("p (m t) -> p t m", t=PACK))
@@ -126,42 +126,71 @@ def tile_picked_zfp_relu_po_kernel(tc, x_words, x_scales, w1, w2_words, w2_scale
         def weight(w, t):
             return dict(lhsT=w_code[w][:, t].bitcast(FP4X4), lhsT_scale=w_scale[:, w, t, :])
 
-        part = [tile([P, PACK, V], F32, "part%d" % d) for d in range(D)]
         halves = [slice(u * VH, (u + 1) * VH) for u in range(HALVES)]
+        part0 = tile([P, PACK, V], F32, "part0")
+        part1 = [tile([P, PACK, VH], F32, "part1_%d" % u) for u in range(HALVES)]
+        e_bf = tile([P, V * PACK], BF16, "e_bf")
 
-        def gather(t, d, cols):
-            offsets = pos_t[d][:, cols.start // 16 : cols.stop // 16]
-            nc.vector.tensor_tensor(part[d][:, t, cols], h[t][:].indirect(offsets), gate_t[d][:, cols], MULT)
+        def gather(t):
+            nc.vector.tensor_tensor(part0[:, t, :], h[t][:].indirect(pos_t[0][:]), gate_t[0], MULT)
 
-        for t in range(PACK - 1):
-            for d in range(D):
-                gather(t, d, slice(0, V))
+        def round_e(copy, u):
+            cols = halves[u]
+            copy(
+                e_bf[:, cols.start * PACK : cols.stop * PACK].rearrange("p (c i j) -> p c j i", i=RUN, j=PACK),
+                e_raw[u].rearrange("p j (c i) -> p c j i", i=RUN),
+            )
+
+        near = [tile([P, PACK, VH], F32, "near0")]
+
+        def fetch(u):
+            cols = halves[u]
+            for t in range(PACK):
+                nc.scalar.activation(near[u][:, t, :], h[t][:].indirect(pos_t[1][:, cols.start // 16 : cols.stop // 16]), COPY)
+
+        def gate_near(u, tiles):
+            count = tiles.stop - tiles.start
+            nc.vector.tensor_tensor(part1[u][:, tiles, :], near[u][:, tiles, :], gate_t[1][:, halves[u]].unsqueeze(1).to_broadcast([P, count, VH]), MULT)
+
+        for t in range(PACK):
+            gather(t)
+        round_e(nc.vector.tensor_copy, 1)
+        fetch(0)
+        round_e(nc.scalar.copy, 0)
+        near.append(over_e.tile([P, PACK, VH], F32, name="near1", offset=0, align_bytes=64))
+        fetch(1)
+        gate_near(0, slice(0, PACK))
         e_code = tile([P, V], U32, "e_code", tag="w_word_raw%d" % W3)
         e_scale = tile([P, V], U8, "e_scale")
         nc.vector.quantize_mx(e_code[:].bitcast(FP8X4), e_scale[:], e_bf[:])
-        gather(PACK - 1, 0, slice(0, V))
-        for cols in halves:
-            gather(PACK - 1, 1, cols)
 
-        acc = [[banks[(PACK * (u + 1) + t) % 8][:, 0:VH] for t in range(PACK)] for u in range(HALVES)]
-        for bank, cols in ((banks[7], slice(0, V)), (banks[6], halves[0])):
-            nc.tensor.matmul_mx(bank[:, cols], rhs=e_code[:, cols].bitcast(FP8X4), rhs_scale=e_scale[:, cols], start=True, stop=True, **weight(W3, 0))
+        acc = [[banks[PACK * u + t][:, 0:VH] for t in range(PACK)] for u in range(HALVES)]
         for u, cols in enumerate(halves):
             for t in range(PACK):
                 nc.tensor.matmul_mx(acc[u][t], rhs=e_code[:, cols].bitcast(FP8X4), rhs_scale=e_scale[:, cols], start=True, stop=False, **weight(W3, t))
 
         z_bf = [tile([P, VH * PACK], BF16, "z_bf%d" % u) for u in range(HALVES)]
-        for u, cols in enumerate(halves):
-            nc.vector.tensor_tensor(
-                z_bf[u][:].rearrange("p (c i t) -> p c t i", i=RUN, t=PACK),
-                part[0][:, :, cols].rearrange("p t (c i) -> p c t i", i=RUN),
-                part[1][:, :, cols].rearrange("p t (c i) -> p c t i", i=RUN),
-                ADD,
-            )
         z_code = [tile([P, VH], U32, "z_code%d" % u) for u in range(HALVES)]
         z_scale = [tile([P, VH], U8, "z_scale%d" % u) for u in range(HALVES)]
-        for u in range(HALVES):
+
+        def add_parts(u):
+            cols = halves[u]
+            nc.vector.tensor_tensor(
+                z_bf[u][:].rearrange("p (c i t) -> p c t i", i=RUN, t=PACK),
+                part0[:, :, cols].rearrange("p t (c i) -> p c t i", i=RUN),
+                part1[u][:].rearrange("p t (c i) -> p c t i", i=RUN),
+                ADD,
+            )
+
+        def quantise_z(u):
             nc.vector.quantize_mx(z_code[u][:].bitcast(FP8X4), z_scale[u][:], z_bf[u][:])
+
+        add_parts(0)
+        gate_near(1, slice(0, PACK - 1))
+        gate_near(1, slice(PACK - 1, PACK))
+        quantise_z(0)
+        add_parts(1)
+        quantise_z(1)
 
         y_code = tile([P, V], U32, "y_code")
         y_scale = tile([P, V], U8, "y_scale")
@@ -171,7 +200,7 @@ def tile_picked_zfp_relu_po_kernel(tc, x_words, x_scales, w1, w2_words, w2_scale
         for u, cols in enumerate(halves):
             for t in range(PACK):
                 nc.tensor.matmul_mx(acc[u][t], rhs=z_code[u][:].bitcast(FP8X4), rhs_scale=z_scale[u][:], start=False, stop=True, **weight(W2, t))
-                if t % 2 == 0:
+                if u == 1 and t % 2 == 0:
                     nc.vector.tensor_scalar(y[u][:, t, :], acc[u][t], 0.0, None, MAX)
                 else:
                     nc.scalar.activation(y[u][:, t, :], acc[u][t], RELU)

@@ -27,7 +27,7 @@ RUN = 4
 VH = 128
 HALVES = V // VH
 W2, W3 = 0, 1
-AT_W3_CODE, AT_W_SCALE, AT_W1_SCALE = 0, 2 * N, 3 * N
+AT_W3_CODE, AT_W_SCALE, AT_W1_SCALE, AT_W2_CODE = 0, 2 * N, 3 * N, 4 * N
 
 
 def tile_picked_zfp_relu_po_kernel(tc, x_words, x_scales, w1, w2_words, w2_scales, gate, eT, w3_words, w3_scales, offs, pos1, pos2, out_0, out_1, out_2):
@@ -85,16 +85,17 @@ def tile_picked_zfp_relu_po_kernel(tc, x_words, x_scales, w1, w2_words, w2_scale
 
         w1_bf = [tile([P, 2, P, PACK], BF16, "w1_bf%d" % a) for a in range(2)]
 
-        def deal_w1(copy, a, c):
+        def deal_w1(copy, a, c, places):
             copy(
-                w1_bf[a][:, :, P // 2 * c : P // 2 * (c + 1), :].rearrange("p b m j -> p m j b"),
-                w1_raw[c][:].rearrange("p j (m t) -> p m j t", t=PACK)[:, :, :, 2 * a : 2 * a + 2],
+                w1_bf[a][:, :, P // 2 * c + places.start : P // 2 * c + places.stop, :].rearrange("p b m j -> p m j b"),
+                w1_raw[c][:].rearrange("p j (m t) -> p m j t", t=PACK)[:, places, :, 2 * a : 2 * a + 2],
             )
 
-        deal_w1(lambda out, in_: nc.scalar.activation(out, in_, COPY), 0, 0)
-        deal_w1(nc.scalar.copy, 1, 0)
-        deal_w1(nc.scalar.copy, 0, 1)
-        deal_w1(nc.vector.tensor_copy, 1, 1)
+        deal_w1(lambda out, in_: nc.scalar.activation(out, in_, COPY), 0, 0, slice(0, P // 2))
+        deal_w1(nc.scalar.copy, 1, 0, slice(0, P // 2))
+        for a in range(2):
+            deal_w1(nc.scalar.copy, a, 1, slice(0, P // 4))
+            deal_w1(nc.vector.tensor_copy, a, 1, slice(P // 4, P // 2))
 
         banks = [ps.tile([P, S], F32, name="bank%d" % b) for b in range(8)]
 
@@ -119,7 +120,7 @@ def tile_picked_zfp_relu_po_kernel(tc, x_words, x_scales, w1, w2_words, w2_scale
                 w_scale[32 * q : 32 * q + 4].rearrange("p w t m -> p (w t m)").bitcast(I32),
                 w_scale_dealt[8 * q : 8 * q + 8].rearrange("p t m -> p (t m)").bitcast(I32),
             )
-        w_code = [tile([P, PACK, P], U16, "w2_code"), on_raw_w1([P, PACK, P], U16, "w3_code", AT_W3_CODE)]
+        w_code = [on_raw_w1([P, PACK, P], U16, "w2_code", AT_W2_CODE), on_raw_w1([P, PACK, P], U16, "w3_code", AT_W3_CODE)]
         for w in (W2, W3):
             nc.vector.tensor_copy(w_code[w][:], w_word_raw[w][:].bitcast(U16).rearrange("p (m t) -> p t m", t=PACK))
 
@@ -128,7 +129,7 @@ def tile_picked_zfp_relu_po_kernel(tc, x_words, x_scales, w1, w2_words, w2_scale
 
         halves = [slice(u * VH, (u + 1) * VH) for u in range(HALVES)]
         part0 = tile([P, PACK, V], F32, "part0")
-        part1 = [tile([P, PACK, VH], F32, "part1_%d" % u) for u in range(HALVES)]
+        part1 = []
         e_bf = tile([P, V * PACK], BF16, "e_bf")
 
         def gather(t):
@@ -143,9 +144,9 @@ def tile_picked_zfp_relu_po_kernel(tc, x_words, x_scales, w1, w2_words, w2_scale
 
         near = [tile([P, PACK, VH], F32, "near0")]
 
-        def fetch(u):
+        def fetch(u, first):
             cols = halves[u]
-            for t in range(PACK):
+            for t in range(first, PACK):
                 nc.scalar.activation(near[u][:, t, :], h[t][:].indirect(pos_t[1][:, cols.start // 16 : cols.stop // 16]), COPY)
 
         def gate_near(u, tiles):
@@ -155,11 +156,13 @@ def tile_picked_zfp_relu_po_kernel(tc, x_words, x_scales, w1, w2_words, w2_scale
         for t in range(PACK):
             gather(t)
         round_e(nc.vector.tensor_copy, 1)
-        fetch(0)
+        fetch(0, 0)
         round_e(nc.scalar.copy, 0)
         near.append(over_e.tile([P, PACK, VH], F32, name="near1", offset=0, align_bytes=64))
-        fetch(1)
+        fetch(1, 1)
+        part1.append(tile([P, PACK, VH], F32, "part1_0", tag="e_raw1"))
         gate_near(0, slice(0, PACK))
+        part1.append(tile([P, PACK, VH], F32, "part1_1", tag="near0"))
         e_code = tile([P, V], U32, "e_code", tag="w_word_raw%d" % W3)
         e_scale = tile([P, V], U8, "e_scale")
         nc.vector.quantize_mx(e_code[:].bitcast(FP8X4), e_scale[:], e_bf[:])
@@ -186,9 +189,10 @@ def tile_picked_zfp_relu_po_kernel(tc, x_words, x_scales, w1, w2_words, w2_scale
             nc.vector.quantize_mx(z_code[u][:].bitcast(FP8X4), z_scale[u][:], z_bf[u][:])
 
         add_parts(0)
-        gate_near(1, slice(0, PACK - 1))
-        gate_near(1, slice(PACK - 1, PACK))
+        nc.vector.tensor_tensor(part1[1][:, 0, :], h[0][:].indirect(pos_t[1][:, VH // 16 : V // 16]), gate_t[1][:, halves[1]], MULT)
         quantise_z(0)
+        gate_near(1, slice(1, PACK - 1))
+        gate_near(1, slice(PACK - 1, PACK))
         add_parts(1)
         quantise_z(1)
 
@@ -197,6 +201,7 @@ def tile_picked_zfp_relu_po_kernel(tc, x_words, x_scales, w1, w2_words, w2_scale
         out_rows = out_0.rearrange("(p t) v -> p t v", t=PACK)
         out_words = out_1[0].rearrange("p c r -> p (c r)").bitcast(I32)
         y = [tile([P, PACK, VH], F32, "y%d" % u) for u in range(HALVES)]
+        y_bf = [tile([P, VH * PACK], BF16, "y_bf%d" % u) for u in range(HALVES)]
         for u, cols in enumerate(halves):
             for t in range(PACK):
                 nc.tensor.matmul_mx(acc[u][t], rhs=z_code[u][:].bitcast(FP8X4), rhs_scale=z_scale[u][:], start=False, stop=True, **weight(W2, t))
@@ -206,10 +211,8 @@ def tile_picked_zfp_relu_po_kernel(tc, x_words, x_scales, w1, w2_words, w2_scale
                     nc.scalar.activation(y[u][:, t, :], acc[u][t], RELU)
             queue = nc.sync if u == 0 else nc.scalar
             queue.dma_start(out_rows[:, :, cols], y[u][:])
+            (nc.scalar.copy if u == 0 else nc.vector.tensor_copy)(y_bf[u][:].rearrange("p (c i t) -> p c t i", i=RUN, t=PACK), y[u][:].rearrange("p t (c i) -> p c t i", i=RUN))
 
-        y_bf = [tile([P, VH * PACK], BF16, "y_bf%d" % u) for u in range(HALVES)]
-        for u in range(HALVES):
-            nc.vector.tensor_copy(y_bf[u][:].rearrange("p (c i t) -> p c t i", i=RUN, t=PACK), y[u][:].rearrange("p t (c i) -> p c t i", i=RUN))
         for u, cols in enumerate(halves):
             nc.vector.quantize_mx(y_code[:, cols].bitcast(FP8X4), y_scale[:, cols], y_bf[u][:])
             nc.sync.dma_start(out_words[:, cols], y_code[:, cols].bitcast(I32))

@@ -35,7 +35,6 @@ def tile_picked_zfp_relu_po_kernel(tc, x_words, x_scales, w1, w2_words, w2_scale
     with ExitStack() as ctx:
         sb = ctx.enter_context(tc.tile_pool(name="sb", bufs=1))
         over = ctx.enter_context(tc.tile_pool(name="over", bufs=1))
-        over_e = ctx.enter_context(tc.tile_pool(name="over_e", bufs=1))
         ps = ctx.enter_context(tc.psum_pool(name="ps", bufs=1))
 
         def tile(shape, dtype, name, tag=None):
@@ -74,7 +73,7 @@ def tile_picked_zfp_relu_po_kernel(tc, x_words, x_scales, w1, w2_words, w2_scale
         nc.sync.dma_start(gates[:], gate.rearrange("d p v -> p d v"))
         gate_t = [gates[:, d, :] for d in range(D)]
         e_rows = eT.rearrange("(p j) v -> p j v", j=PACK)
-        e_raw = [over_e.tile([P, PACK, VH], F32, name="e_raw0", offset=0, align_bytes=64)[:], tile([P, PACK, VH], F32, "e_raw1")[:]]
+        e_raw = [tile([P, PACK, VH], F32, "e_raw%d" % u)[:] for u in range(HALVES)]
         for u in range(HALVES):
             nc.sync.dma_start(e_raw[u], e_rows[:, :, u * VH : (u + 1) * VH])
 
@@ -129,89 +128,71 @@ def tile_picked_zfp_relu_po_kernel(tc, x_words, x_scales, w1, w2_words, w2_scale
 
         halves = [slice(u * VH, (u + 1) * VH) for u in range(HALVES)]
         part0 = tile([P, PACK, V], F32, "part0")
-        part1 = []
-        e_bf = tile([P, V * PACK], BF16, "e_bf")
-
-        def gather(t):
+        for t in range(PACK):
             nc.vector.tensor_tensor(part0[:, t, :], h[t][:].indirect(pos_t[0][:]), gate_t[0], MULT)
-
-        def round_e(copy, u):
-            cols = halves[u]
-            copy(
-                e_bf[:, cols.start * PACK : cols.stop * PACK].rearrange("p (c i j) -> p c j i", i=RUN, j=PACK),
-                e_raw[u].rearrange("p j (c i) -> p c j i", i=RUN),
-            )
-
-        near = [tile([P, PACK, VH], F32, "near0")]
-
-        def fetch(u, first):
-            cols = halves[u]
-            for t in range(first, PACK):
+        near = [tile([P, PACK, VH], F32, "near%d" % u) for u in range(HALVES)]
+        for u, cols in enumerate(halves):
+            for t in range(PACK):
                 nc.scalar.activation(near[u][:, t, :], h[t][:].indirect(pos_t[1][:, cols.start // 16 : cols.stop // 16]), COPY)
+
+        e_bf = [tile([P, VH * PACK], BF16, "e_bf0"), tile([P, VH * PACK], BF16, "e_bf1", tag="h3")]
+        for u, copy in enumerate((nc.vector.tensor_copy, nc.scalar.copy)):
+            copy(e_bf[u][:].rearrange("p (c i j) -> p c j i", i=RUN, j=PACK), e_raw[u].rearrange("p j (c i) -> p c j i", i=RUN))
+        part1 = [tile([P, PACK, VH], F32, "part1_0")]
 
         def gate_near(u, tiles):
             count = tiles.stop - tiles.start
             nc.vector.tensor_tensor(part1[u][:, tiles, :], near[u][:, tiles, :], gate_t[1][:, halves[u]].unsqueeze(1).to_broadcast([P, count, VH]), MULT)
 
-        for t in range(PACK):
-            gather(t)
-        round_e(nc.vector.tensor_copy, 1)
-        fetch(0, 0)
-        round_e(nc.scalar.copy, 0)
-        near.append(over_e.tile([P, PACK, VH], F32, name="near1", offset=0, align_bytes=64))
-        fetch(1, 1)
-        part1.append(tile([P, PACK, VH], F32, "part1_0", tag="e_raw1"))
-        gate_near(0, slice(0, PACK))
-        part1.append(tile([P, PACK, VH], F32, "part1_1", tag="near0"))
-        e_code = tile([P, V], U32, "e_code", tag="w_word_raw%d" % W3)
-        e_scale = tile([P, V], U8, "e_scale")
-        nc.vector.quantize_mx(e_code[:].bitcast(FP8X4), e_scale[:], e_bf[:])
-
         acc = [[banks[PACK * u + t][:, 0:VH] for t in range(PACK)] for u in range(HALVES)]
-        for u, cols in enumerate(halves):
-            for t in range(PACK):
-                nc.tensor.matmul_mx(acc[u][t], rhs=e_code[:, cols].bitcast(FP8X4), rhs_scale=e_scale[:, cols], start=True, stop=False, **weight(W3, t))
-
-        z_bf = [tile([P, VH * PACK], BF16, "z_bf%d" % u) for u in range(HALVES)]
-        z_code = [tile([P, VH], U32, "z_code%d" % u) for u in range(HALVES)]
-        z_scale = [tile([P, VH], U8, "z_scale%d" % u) for u in range(HALVES)]
-
-        def add_parts(u):
-            cols = halves[u]
-            nc.vector.tensor_tensor(
-                z_bf[u][:].rearrange("p (c i t) -> p c t i", i=RUN, t=PACK),
-                part0[:, :, cols].rearrange("p t (c i) -> p c t i", i=RUN),
-                part1[u][:].rearrange("p t (c i) -> p c t i", i=RUN),
-                ADD,
-            )
-
-        def quantise_z(u):
-            nc.vector.quantize_mx(z_code[u][:].bitcast(FP8X4), z_scale[u][:], z_bf[u][:])
-
-        add_parts(0)
-        nc.vector.tensor_tensor(part1[1][:, 0, :], h[0][:].indirect(pos_t[1][:, VH // 16 : V // 16]), gate_t[1][:, halves[1]], MULT)
-        quantise_z(0)
-        gate_near(1, slice(1, PACK - 1))
-        gate_near(1, slice(PACK - 1, PACK))
-        add_parts(1)
-        quantise_z(1)
-
         y_code = tile([P, V], U32, "y_code")
         y_scale = tile([P, V], U8, "y_scale")
         out_rows = out_0.rearrange("(p t) v -> p t v", t=PACK)
         out_words = out_1[0].rearrange("p c r -> p (c r)").bitcast(I32)
-        y = [tile([P, PACK, VH], F32, "y%d" % u) for u in range(HALVES)]
         y_bf = [tile([P, VH * PACK], BF16, "y_bf%d" % u) for u in range(HALVES)]
-        for u, cols in enumerate(halves):
+
+        def multiply_e(u):
+            code = tile([P, VH], U32, "e_code%d" % u)
+            scale = tile([P, VH], U8, "e_scale%d" % u, tag="z_bf0" if u == 1 else None)
+            nc.vector.quantize_mx(code[:].bitcast(FP8X4), scale[:], e_bf[u][:])
             for t in range(PACK):
-                nc.tensor.matmul_mx(acc[u][t], rhs=z_code[u][:].bitcast(FP8X4), rhs_scale=z_scale[u][:], start=False, stop=True, **weight(W2, t))
-                if u == 1 and t % 2 == 0:
-                    nc.vector.tensor_scalar(y[u][:, t, :], acc[u][t], 0.0, None, MAX)
+                nc.tensor.matmul_mx(acc[u][t], rhs=code[:].bitcast(FP8X4), rhs_scale=scale[:], start=True, stop=False, **weight(W3, t))
+
+        def add_parts(u):
+            z_bf = tile([P, VH * PACK], BF16, "z_bf%d" % u)
+            nc.vector.tensor_tensor(
+                z_bf[:].rearrange("p (c i t) -> p c t i", i=RUN, t=PACK),
+                part0[:, :, halves[u]].rearrange("p t (c i) -> p c t i", i=RUN),
+                part1[u][:].rearrange("p t (c i) -> p c t i", i=RUN),
+                ADD,
+            )
+            return z_bf
+
+        def multiply_z(u, z_bf):
+            code = tile([P, VH], U32, "z_code%d" % u)
+            scale = tile([P, VH], U8, "z_scale%d" % u)
+            nc.vector.quantize_mx(code[:].bitcast(FP8X4), scale[:], z_bf[:])
+            y = tile([P, PACK, VH], F32, "y%d" % u)
+            for t in range(PACK):
+                nc.tensor.matmul_mx(acc[u][t], rhs=code[:].bitcast(FP8X4), rhs_scale=scale[:], start=False, stop=True, **weight(W2, t))
+                if u == 1 and t < 2:
+                    nc.vector.tensor_scalar(y[:, t, :], acc[u][t], 0.0, None, MAX)
                 else:
-                    nc.scalar.activation(y[u][:, t, :], acc[u][t], RELU)
+                    nc.scalar.activation(y[:, t, :], acc[u][t], RELU)
             queue = nc.sync if u == 0 else nc.scalar
-            queue.dma_start(out_rows[:, :, cols], y[u][:])
-            (nc.scalar.copy if u == 0 else nc.vector.tensor_copy)(y_bf[u][:].rearrange("p (c i t) -> p c t i", i=RUN, t=PACK), y[u][:].rearrange("p t (c i) -> p c t i", i=RUN))
+            queue.dma_start(out_rows[:, :, halves[u]], y[:])
+            copy = nc.scalar.copy if u == 0 else nc.vector.tensor_copy
+            copy(y_bf[u][:].rearrange("p (c i t) -> p c t i", i=RUN, t=PACK), y[:].rearrange("p t (c i) -> p c t i", i=RUN))
+
+        gate_near(0, slice(0, PACK))
+        multiply_e(0)
+        part1.append(tile([P, PACK, VH], F32, "part1_1", tag="e_bf0"))
+        z_bf0 = add_parts(0)
+        gate_near(1, slice(0, PACK - 1))
+        multiply_z(0, z_bf0)
+        gate_near(1, slice(PACK - 1, PACK))
+        multiply_e(1)
+        multiply_z(1, add_parts(1))
 
         for u, cols in enumerate(halves):
             nc.vector.quantize_mx(y_code[:, cols].bitcast(FP8X4), y_scale[:, cols], y_bf[u][:])

@@ -157,6 +157,9 @@ def tile_picked_zfp_relu_po_kernel(tc, x_words, x_scales, w1, w2_words, w2_scale
             nc.vector.quantize_mx(code[:].bitcast(FP8X4), scale[:], e_bf[u][:])
             for t in range(PACK):
                 nc.tensor.matmul_mx(acc[u][t], rhs=code[:].bitcast(FP8X4), rhs_scale=scale[:], start=True, stop=False, **weight(W3, t))
+            if u == 0:
+                for t in range(1, PACK):
+                    nc.tensor.matmul_mx(acc[1][t], rhs=code[:].bitcast(FP8X4), rhs_scale=scale[:], start=True, stop=True, **weight(W3, t))
 
         def add_parts(u):
             z_bf = tile([P, VH * PACK], BF16, "z_bf%d" % u)

@@ -130,15 +130,20 @@ def tile_picked_zfp_relu_po_kernel(tc, x_words, x_scales, w1, w2_words, w2_scale
         part0 = tile([P, PACK, V], F32, "part0")
         for t in range(PACK):
             nc.vector.tensor_tensor(part0[:, t, :], h[t][:].indirect(pos_t[0][:]), gate_t[0], MULT)
-        near = [tile([P, PACK, VH], F32, "near%d" % u) for u in range(HALVES)]
+        e_bf = [tile([P, VH * PACK], BF16, "e_bf0")]
+        near = []
         for u, cols in enumerate(halves):
-            for t in range(PACK):
+            near.append(tile([P, PACK, VH], F32, "near%d" % u))
+            for t in range(1, PACK):
                 nc.scalar.activation(near[u][:, t, :], h[t][:].indirect(pos_t[1][:, cols.start // 16 : cols.stop // 16]), COPY)
-
-        e_bf = [tile([P, VH * PACK], BF16, "e_bf0"), tile([P, VH * PACK], BF16, "e_bf1", tag="h3")]
-        for u, copy in enumerate((nc.vector.tensor_copy, nc.scalar.copy)):
-            copy(e_bf[u][:].rearrange("p (c i j) -> p c j i", i=RUN, j=PACK), e_raw[u].rearrange("p j (c i) -> p c j i", i=RUN))
+            if u == 1:
+                e_bf.append(tile([P, VH * PACK], BF16, "e_bf1", tag="h2"))
+            nc.scalar.copy(e_bf[u][:].rearrange("p (c i j) -> p c j i", i=RUN, j=PACK), e_raw[u].rearrange("p j (c i) -> p c j i", i=RUN))
         part1 = [tile([P, PACK, VH], F32, "part1_0")]
+
+        def gather_second(u):
+            cols = halves[u]
+            nc.vector.tensor_tensor(part1[u][:, 0, :], h[0][:].indirect(pos_t[1][:, cols.start // 16 : cols.stop // 16]), gate_t[1][:, cols], MULT)
 
         def gate_near(u, tiles):
             count = tiles.stop - tiles.start
@@ -187,12 +192,14 @@ def tile_picked_zfp_relu_po_kernel(tc, x_words, x_scales, w1, w2_words, w2_scale
             copy = nc.scalar.copy if u == 0 else nc.vector.tensor_copy
             copy(y_bf[u][:].rearrange("p (c i t) -> p c t i", i=RUN, t=PACK), y[:].rearrange("p t (c i) -> p c t i", i=RUN))
 
-        gate_near(0, slice(0, PACK))
+        gather_second(0)
+        gate_near(0, slice(1, PACK))
         multiply_e(0)
         part1.append(tile([P, PACK, VH], F32, "part1_1", tag="e_bf0"))
         z_bf0 = add_parts(0)
-        gate_near(1, slice(0, PACK - 1))
+        gather_second(1)
         multiply_z(0, z_bf0)
+        gate_near(1, slice(1, PACK - 1))
         gate_near(1, slice(PACK - 1, PACK))
         multiply_e(1)
         multiply_z(1, add_parts(1))

@@ -149,7 +149,7 @@ def tile_picked_zfp_relu_po_kernel(tc, x_words, x_scales, w1, w2_words, w2_scale
             count = tiles.stop - tiles.start
             nc.vector.tensor_tensor(part1[u][:, tiles, :], near[u][:, tiles, :], gate_t[1][:, halves[u]].unsqueeze(1).to_broadcast([P, count, VH]), MULT)
 
-        acc = [[banks[PACK * u + t][:, 0:VH] for t in range(PACK)] for u in range(HALVES)]
+        acc = [[banks[0][:, t * VH : (t + 1) * VH] for t in range(PACK)], [banks[PACK + t][:, 0:VH] for t in range(PACK)]]
         y_code = tile([P, V], U32, "y_code")
         y_scale = tile([P, V], U8, "y_scale")
         out_rows = out_0.rearrange("(p t) v -> p t v", t=PACK)
@@ -161,7 +161,7 @@ def tile_picked_zfp_relu_po_kernel(tc, x_words, x_scales, w1, w2_words, w2_scale
             scale = tile([P, VH], U8, "e_scale%d" % u, tag="z_bf0" if u == 1 else None)
             nc.vector.quantize_mx(code[:].bitcast(FP8X4), scale[:], e_bf[u][:])
             for t in range(PACK):
-                nc.tensor.matmul_mx(acc[u][t], rhs=code[:].bitcast(FP8X4), rhs_scale=scale[:], start=True, stop=False, **weight(W3, t))
+                nc.tensor.matmul_mx(acc[u][t], rhs=code[:].bitcast(FP8X4), rhs_scale=scale[:], start=(u == 1 or t == 0), stop=False, **weight(W3, t))
             if u == 0:
                 for t in range(1, PACK):
                     nc.tensor.matmul_mx(acc[1][t], rhs=code[:].bitcast(FP8X4), rhs_scale=scale[:], start=True, stop=True, **weight(W3, t))
@@ -181,16 +181,20 @@ def tile_picked_zfp_relu_po_kernel(tc, x_words, x_scales, w1, w2_words, w2_scale
             scale = tile([P, VH], U8, "z_scale%d" % u)
             nc.vector.quantize_mx(code[:].bitcast(FP8X4), scale[:], z_bf[:])
             y = tile([P, PACK, VH], F32, "y%d" % u)
+            woven = y_bf[u][:].rearrange("p (c i t) -> p c t i", i=RUN, t=PACK)
             for t in range(PACK):
-                nc.tensor.matmul_mx(acc[u][t], rhs=code[:].bitcast(FP8X4), rhs_scale=scale[:], start=False, stop=True, **weight(W2, t))
+                nc.tensor.matmul_mx(acc[u][t], rhs=code[:].bitcast(FP8X4), rhs_scale=scale[:], start=False, stop=(u == 1 or t == PACK - 1), **weight(W2, t))
                 if u == 1 and t < 2:
                     nc.vector.tensor_scalar(y[:, t, :], acc[u][t], 0.0, None, MAX)
-                else:
+                elif u == 1:
                     nc.scalar.activation(y[:, t, :], acc[u][t], RELU)
-            queue = nc.sync if u == 0 else nc.scalar
-            queue.dma_start(out_rows[:, :, halves[u]], y[:])
-            copy = nc.scalar.copy if u == 0 else nc.vector.tensor_copy
-            copy(y_bf[u][:].rearrange("p (c i t) -> p c t i", i=RUN, t=PACK), y[:].rearrange("p t (c i) -> p c t i", i=RUN))
+            if u == 0:
+                nc.scalar.activation(y[:].rearrange("p t v -> p (t v)"), banks[0][:], RELU)
+                nc.sync.dma_start(out_rows[:, :, halves[u]], y[:])
+                nc.scalar.activation(woven, banks[0][:].rearrange("p (t c i) -> p c t i", t=PACK, i=RUN), RELU)
+            else:
+                nc.scalar.dma_start(out_rows[:, :, halves[u]], y[:])
+                nc.vector.tensor_copy(woven, y[:].rearrange("p t (c i) -> p c t i", i=RUN))
 
         gather_second(0)
         gate_near(0, slice(1, PACK))

@@ -184,7 +184,7 @@ def tile_picked_zfp_relu_po_kernel(tc, x_words, x_scales, w1, w2_words, w2_scale
             woven = y_bf[u][:].rearrange("p (c i t) -> p c t i", i=RUN, t=PACK)
             for t in range(PACK):
                 nc.tensor.matmul_mx(acc[u][t], rhs=code[:].bitcast(FP8X4), rhs_scale=scale[:], start=False, stop=(u == 1 or t == PACK - 1), **weight(W2, t))
-                if u == 1 and t < 2:
+                if u == 1 and t % 2 == 0:
                     nc.vector.tensor_scalar(y[:, t, :], acc[u][t], 0.0, None, MAX)
                 elif u == 1:
                     nc.scalar.activation(y[:, t, :], acc[u][t], RELU)

@@ -38,10 +38,10 @@ def tile_picked_zfp_relu_po_kernel(tc, x_words, x_scales, w1, w2_words, w2_scale
         ps = ctx.enter_context(tc.psum_pool(name="ps", bufs=1))
 
         def tile(shape, dtype, name, tag=None):
-            return sb.tile(shape, dtype, name=name, tag=tag or name, align_bytes=64)
+            return sb.tile(shape, dtype, name=name, tag=tag or name, align_bytes=256)
 
-        def on_raw_w1(shape, dtype, name, offset):
-            return over.tile(shape, dtype, name=name, offset=offset, align_bytes=64)
+        def on_raw_w1(shape, dtype, name, offset, align=64):
+            return over.tile(shape, dtype, name=name, offset=offset, align_bytes=align)
 
         offs_t = sb.tile([P, S // 16], U16, name="offs_t")
         pos_t = [sb.tile([P, V // 16], U16, name="pos_t%d" % d) for d in range(D)]
@@ -56,9 +56,9 @@ def tile_picked_zfp_relu_po_kernel(tc, x_words, x_scales, w1, w2_words, w2_scale
         x_word_tab = tile([P, T], I32, "x_word_tab")
         nc.sync.dma_start(x_word_tab[:], x_words[0].rearrange("p c r -> p (c r)").bitcast(I32))
         nc.sync.dma_start(offs_t[:], offs)
-        for q in range(QUADS):
-            nc.sync.dma_start(x_scale_tab[32 * q : 32 * q + 4, :].bitcast(I32), x_scales[0, 4 * q : 4 * q + 4, :].bitcast(I32))
-        w1_raw = [tile([P, PACK, H // 2], F32, "w1_raw0"), on_raw_w1([P, PACK, H // 2], F32, "w1_raw1", 0)]
+        for r in range(PACK):
+            nc.sync.dma_start(x_scale_tab[r : P : 32, :].bitcast(I32), x_scales[0, r : ROWS : PACK, :].bitcast(I32))
+        w1_raw = [tile([P, PACK, H // 2], F32, "w1_raw0"), on_raw_w1([P, PACK, H // 2], F32, "w1_raw1", 0, align=256)]
         w1_rows = w1.rearrange("(p j) c -> p j c", j=PACK)
         for c in range(2):
             nc.sync.dma_start(w1_raw[c][:], w1_rows[:, :, c * (H // 2) : (c + 1) * (H // 2)])

from contextlib import ExitStack

import concourse.mybir as mybir

K, T, S, D, V, H, N = 512, 1024, 512, 2, 256, 512, 512
FLOPS = 2 * K * H * S + 2 * H * N * V + 2 * K * N * V

F32 = mybir.dt.float32
BF16 = mybir.dt.bfloat16
I32 = mybir.dt.int32
U32 = mybir.dt.uint32
U16 = mybir.dt.uint16
U8 = mybir.dt.uint8
FP8X4 = mybir.dt.float8_e4m3fn_x4
FP4X4 = mybir.dt.float4_e2m1fn_x4
RELU = mybir.ActivationFunctionType.Relu
COPY = mybir.ActivationFunctionType.Copy
MULT = mybir.AluOpType.mult
ADD = mybir.AluOpType.add
MAX = mybir.AluOpType.max

P = 128
PACK = 4
QUADS = 4
ROWS = 16
RUN = 4
VH = 128
HALVES = V // VH
W2, W3 = 0, 1
AT_W3_CODE, AT_W_SCALE, AT_W1_SCALE, AT_W2_CODE = 0, 2 * N, 3 * N, 4 * N


def tile_picked_zfp_relu_po_kernel(tc, x_words, x_scales, w1, w2_words, w2_scales, gate, eT, w3_words, w3_scales, offs, pos1, pos2, out_0, out_1, out_2):
    nc = tc.nc
    with ExitStack() as ctx:
        sb = ctx.enter_context(tc.tile_pool(name="sb", bufs=1))
        over = ctx.enter_context(tc.tile_pool(name="over", bufs=1))
        ps = ctx.enter_context(tc.psum_pool(name="ps", bufs=1))

        def tile(shape, dtype, name, tag=None):
            return sb.tile(shape, dtype, name=name, tag=tag or name, align_bytes=256)

        def on_raw_w1(shape, dtype, name, offset, align=64):
            return over.tile(shape, dtype, name=name, offset=offset, align_bytes=align)

        offs_t = sb.tile([P, S // 16], U16, name="offs_t")
        pos_t = [sb.tile([P, V // 16], U16, name="pos_t%d" % d) for d in range(D)]

        x_scale_tab = tile([P, T], U8, "x_scale_tab")
        w_scale_raw = tile([P, N], U8, "w_scale_raw")
        w_scale = tile([P, 2, PACK, P], U8, "w_scale")
        nc.gpsimd.memset(x_scale_tab[:].bitcast(I32), 0)
        nc.gpsimd.memset(w_scale_raw[:].bitcast(I32), 0)
        nc.gpsimd.memset(w_scale[:].rearrange("p w t m -> p (w t m)").bitcast(I32), 0)

        x_word_tab = tile([P, T], I32, "x_word_tab")
        nc.sync.dma_start(x_word_tab[:], x_words[0].rearrange("p c r -> p (c r)").bitcast(I32))
        nc.sync.dma_start(offs_t[:], offs)
        for r in range(PACK):
            nc.sync.dma_start(x_scale_tab[r : P : 32, :].bitcast(I32), x_scales[0, r : ROWS : PACK, :].bitcast(I32))
        w1_raw = [tile([P, PACK, H // 2], F32, "w1_raw0"), on_raw_w1([P, PACK, H // 2], F32, "w1_raw1", 0, align=256)]
        w1_rows = w1.rearrange("(p j) c -> p j c", j=PACK)
        for c in range(2):
            nc.sync.dma_start(w1_raw[c][:], w1_rows[:, :, c * (H // 2) : (c + 1) * (H // 2)])
        w_word_raw = [tile([P, 2 * N], U8, "w_word_raw%d" % w) for w in (W2, W3)]
        for w, words in ((W2, w2_words), (W3, w3_words)):
            nc.sync.dma_start(w_word_raw[w][:], words[0])
        for w, scales in ((W2, w2_scales), (W3, w3_scales)):
            nc.sync.dma_start(w_scale_raw[w : 2 * ROWS : 2, :].bitcast(I32), scales[0].bitcast(I32))
        nc.sync.dma_start(pos_t[0][:], pos1)
        nc.sync.dma_start(pos_t[1][:], pos2)
        gates = tile([P, D, V], F32, "gates")
        nc.sync.dma_start(gates[:], gate.rearrange("d p v -> p d v"))
        gate_t = [gates[:, d, :] for d in range(D)]
        e_rows = eT.rearrange("(p j) v -> p j v", j=PACK)
        e_raw = [tile([P, PACK, VH], F32, "e_raw%d" % u)[:] for u in range(HALVES)]
        for u in range(HALVES):
            nc.sync.dma_start(e_raw[u], e_rows[:, :, u * VH : (u + 1) * VH])

        x_scale = tile([P, S], U8, "x_scale")
        x_code = tile([P, S], U32, "x_code")
        nc.vector.tensor_copy(x_code[:], x_word_tab[:].bitcast(U32).indirect(offs_t[:]))
        nc.vector.tensor_copy(x_scale[:], x_scale_tab[:].indirect(offs_t[:]))

        w1_bf = [tile([P, 2, P, PACK], BF16, "w1_bf%d" % a) for a in range(2)]

        def deal_w1(copy, a, c, places):
            copy(
                w1_bf[a][:, :, P // 2 * c + places.start : P // 2 * c + places.stop, :].rearrange("p b m j -> p m j b"),
                w1_raw[c][:].rearrange("p j (m t) -> p m j t", t=PACK)[:, places, :, 2 * a : 2 * a + 2],
            )

        deal_w1(lambda out, in_: nc.scalar.activation(out, in_, COPY), 0, 0, slice(0, P // 2))
        deal_w1(nc.scalar.copy, 1, 0, slice(0, P // 2))
        for a in range(2):
            deal_w1(nc.scalar.copy, a, 1, slice(0, P // 4))
            deal_w1(nc.vector.tensor_copy, a, 1, slice(P // 4, P // 2))

        banks = [ps.tile([P, S], F32, name="bank%d" % b) for b in range(8)]

        def make_h(t, code_tag=None, h_tag=None):
            code = tile([P, P], U32, "w1_code%d" % t, tag=code_tag)
            name = "w1_scale%d" % t
            scale = tile([P, P], U8, name) if t < 2 else on_raw_w1([P, P], U8, name, AT_W1_SCALE + (t - 2) * P)
            nc.vector.quantize_mx(code[:].bitcast(FP8X4), scale[:], w1_bf[t // 2][:, t % 2].rearrange("p m j -> p (m j)"))
            h_t = tile([P, S], F32, "h%d" % t, tag=h_tag)
            for c in range(2):
                bank, cols = banks[2 * t + c], slice(c * S // 2, (c + 1) * S // 2)
                nc.tensor.matmul_mx(bank[:, cols], lhsT=code[:].bitcast(FP8X4), lhsT_scale=scale[:], rhs=x_code[:, cols].bitcast(FP8X4), rhs_scale=x_scale[:, cols], start=True, stop=True)
                nc.scalar.activation(h_t[:, cols], bank[:, cols], RELU)
            return h_t

        h = [make_h(t) for t in range(PACK)]

        w_scale_dealt = on_raw_w1([P, PACK, P], U8, "w_scale_dealt", AT_W_SCALE)
        nc.vector.tensor_copy(w_scale_dealt[:], w_scale_raw[:].rearrange("p (m t) -> p t m", t=PACK))
        for q in range(QUADS):
            nc.sync.dma_start(
                w_scale[32 * q : 32 * q + 4].rearrange("p w t m -> p (w t m)").bitcast(I32),
                w_scale_dealt[8 * q : 8 * q + 8].rearrange("p t m -> p (t m)").bitcast(I32),
            )
        w_code = [on_raw_w1([P, PACK, P], U16, "w2_code", AT_W2_CODE), on_raw_w1([P, PACK, P], U16, "w3_code", AT_W3_CODE)]
        for w in (W2, W3):
            nc.vector.tensor_copy(w_code[w][:], w_word_raw[w][:].bitcast(U16).rearrange("p (m t) -> p t m", t=PACK))

        def weight(w, t):
            return dict(lhsT=w_code[w][:, t].bitcast(FP4X4), lhsT_scale=w_scale[:, w, t, :])

        halves = [slice(u * VH, (u + 1) * VH) for u in range(HALVES)]
        part0 = tile([P, PACK, V], F32, "part0")
        for t in range(PACK):
            nc.vector.tensor_tensor(part0[:, t, :], h[t][:].indirect(pos_t[0][:]), gate_t[0], MULT)
        e_bf = [tile([P, VH * PACK], BF16, "e_bf0")]
        near = []
        for u, cols in enumerate(halves):
            near.append(tile([P, PACK, VH], F32, "near%d" % u))
            for t in range(1, PACK):
                nc.scalar.activation(near[u][:, t, :], h[t][:].indirect(pos_t[1][:, cols.start // 16 : cols.stop // 16]), COPY)
            if u == 1:
                e_bf.append(tile([P, VH * PACK], BF16, "e_bf1", tag="h2"))
            nc.scalar.copy(e_bf[u][:].rearrange("p (c i j) -> p c j i", i=RUN, j=PACK), e_raw[u].rearrange("p j (c i) -> p c j i", i=RUN))
        part1 = [tile([P, PACK, VH], F32, "part1_0")]

        def gather_second(u):
            cols = halves[u]
            nc.vector.tensor_tensor(part1[u][:, 0, :], h[0][:].indirect(pos_t[1][:, cols.start // 16 : cols.stop // 16]), gate_t[1][:, cols], MULT)

        def gate_near(u, tiles):
            count = tiles.stop - tiles.start
            nc.vector.tensor_tensor(part1[u][:, tiles, :], near[u][:, tiles, :], gate_t[1][:, halves[u]].unsqueeze(1).to_broadcast([P, count, VH]), MULT)

        acc = [[banks[0][:, t * VH : (t + 1) * VH] for t in range(PACK)], [banks[PACK + t][:, 0:VH] for t in range(PACK)]]
        y_code = tile([P, V], U32, "y_code")
        y_scale = tile([P, V], U8, "y_scale")
        out_rows = out_0.rearrange("(p t) v -> p t v", t=PACK)
        out_words = out_1[0].rearrange("p c r -> p (c r)").bitcast(I32)
        y_bf = [tile([P, VH * PACK], BF16, "y_bf%d" % u) for u in range(HALVES)]

        def multiply_e(u):
            code = tile([P, VH], U32, "e_code%d" % u)
            scale = tile([P, VH], U8, "e_scale%d" % u, tag="z_bf0" if u == 1 else None)
            nc.vector.quantize_mx(code[:].bitcast(FP8X4), scale[:], e_bf[u][:])
            for t in range(PACK):
                nc.tensor.matmul_mx(acc[u][t], rhs=code[:].bitcast(FP8X4), rhs_scale=scale[:], start=(u == 1 or t == 0), stop=False, **weight(W3, t))
            if u == 0:
                for t in range(1, PACK):
                    nc.tensor.matmul_mx(acc[1][t], rhs=code[:].bitcast(FP8X4), rhs_scale=scale[:], start=True, stop=True, **weight(W3, t))

        def add_parts(u):
            z_bf = tile([P, VH * PACK], BF16, "z_bf%d" % u)
            nc.vector.tensor_tensor(
                z_bf[:].rearrange("p (c i t) -> p c t i", i=RUN, t=PACK),
                part0[:, :, halves[u]].rearrange("p t (c i) -> p c t i", i=RUN),
                part1[u][:].rearrange("p t (c i) -> p c t i", i=RUN),
                ADD,
            )
            return z_bf

        def multiply_z(u, z_bf):
            code = tile([P, VH], U32, "z_code%d" % u)
            scale = tile([P, VH], U8, "z_scale%d" % u)
            nc.vector.quantize_mx(code[:].bitcast(FP8X4), scale[:], z_bf[:])
            y = tile([P, PACK, VH], F32, "y%d" % u)
            woven = y_bf[u][:].rearrange("p (c i t) -> p c t i", i=RUN, t=PACK)
            for t in range(PACK):
                nc.tensor.matmul_mx(acc[u][t], rhs=code[:].bitcast(FP8X4), rhs_scale=scale[:], start=False, stop=(u == 1 or t == PACK - 1), **weight(W2, t))
                if u == 1 and t % 2 == 0:
                    nc.vector.tensor_scalar(y[:, t, :], acc[u][t], 0.0, None, MAX)
                elif u == 1:
                    nc.scalar.activation(y[:, t, :], acc[u][t], RELU)
            if u == 0:
                nc.scalar.activation(y[:].rearrange("p t v -> p (t v)"), banks[0][:], RELU)
                nc.sync.dma_start(out_rows[:, :, halves[u]], y[:])
                nc.scalar.activation(woven, banks[0][:].rearrange("p (t c i) -> p c t i", t=PACK, i=RUN), RELU)
            else:
                nc.scalar.dma_start(out_rows[:, :, halves[u]], y[:])
                nc.vector.tensor_copy(woven, y[:].rearrange("p t (c i) -> p c t i", i=RUN))

        gather_second(0)
        gate_near(0, slice(1, PACK))
        multiply_e(0)
        part1.append(tile([P, PACK, VH], F32, "part1_1", tag="e_bf0"))
        z_bf0 = add_parts(0)
        gather_second(1)
        multiply_z(0, z_bf0)
        gate_near(1, slice(1, PACK - 1))
        gate_near(1, slice(PACK - 1, PACK))
        multiply_e(1)
        multiply_z(1, add_parts(1))

        for u, cols in enumerate(halves):
            nc.vector.quantize_mx(y_code[:, cols].bitcast(FP8X4), y_scale[:, cols], y_bf[u][:])
            nc.sync.dma_start(out_words[:, cols], y_code[:, cols].bitcast(I32))
        for q in range(QUADS):
            queue = nc.scalar if q % 2 == 0 else nc.sync
            queue.dma_start(out_2[0, 4 * q : 4 * q + 4, :].bitcast(I32), y_scale[32 * q : 32 * q + 4, :].bitcast(I32))
